import numpy as np, ml_dtypes
CORES = [10,34,74,98]
N = 4
BF = ml_dtypes.bfloat16
T, NB, C, RO = 4, 11, 2048, 4
V, W, CN = 8 * N * T, 2 ** NB, C // N
def scores(rng):
    w = rng.choice(np.array([0.0, 0.25, 0.5, 0.75], np.float32), (N, 8, T, 1, 1))
    a = rng.integers(0, 256, (N, 8, T, 1, W)).astype(np.float32); b = rng.integers(0, 256, (N, 8, T, 16, W)).astype(np.float32)
    return np.floor(w * a + (1 - w) * b)
def parents(rng):
    return np.argsort(rng.random((V, V)) + 2 * np.eye(V), axis=1)[:, :NB]
def orders(rng):
    return np.argsort(rng.random((V, C)), axis=0)
def full(rng, cd):
    v = int(rng.integers(0, V)); m = rng.permutation(C) & (W - 1)
    key = 2 * rng.random((V, C)); bit = (m[None, :] >> np.arange(NB)[:, None]) & 1
    key[v] = 1.0; key[cd[v]] = 0.9 * rng.random((NB, C)) + 1.1 * (1 - bit)
    return np.argsort(np.argsort(key, axis=0), axis=0)
def moves(rng):
    return 2 * rng.integers(0, V // 2, (RO, C)) + 1, rng.integers(0, V, (RO, C)), rng.integers(0, 18, (RO, C))
def pack(rng, v, cd, p, fa, ic, t):
    t = np.array(t)
    for k in range(N):
        i = k * CN + rng.permutation(CN)[:2]; t[:, i[0]] = 0; t[:, i[1]] = 17
    same = lambda a: np.repeat(np.asarray(a)[None], N, axis=0).astype(np.int32)
    return {"tab": np.ascontiguousarray(v.transpose(0, 1, 3, 2, 4)).reshape(N, 128, T * W).astype(np.float32).astype(BF),
            "cand": np.ascontiguousarray(np.reshape(cd, (N, 8, T * NB))).astype(np.int32),
            "pos0": same(p), "fac": same(fa), "inc": same(ic), "th": same(t)}
def setup_inputs(rng):
    fa, ic, t = moves(rng)
    t = np.where(rng.random((RO, C)) < 0.7, rng.integers(5, 12, (RO, C)), t)
    return pack(rng, scores(rng), parents(rng), orders(rng), fa, ic, t)
def setup_inputs_ties(rng):
    v = rng.integers(0, 2 + rng.integers(0, 2, (N, 8, T, 1, 1)), (N, 8, T, 16, W))
    fa, ic, t = moves(rng); u = rng.integers(0, 3, (RO, C))
    fa = np.where(u < 2, 1, fa); ic = np.where(u == 0, 0, ic)
    t = np.where(rng.random((RO, C)) < 0.6, rng.choice(np.array([1, 8, 15, 16, 17]), (RO, C)), t)
    o = rng.permutation(V); b = V // 16; cd = np.empty((V, NB), np.int64); p = np.empty((V, C), np.int64)
    j = np.argsort(rng.random((V, 16)) + 2 * np.tile(np.eye(16), (b, 1)), axis=1)[:, :NB]
    cd[o] = o[16 * (np.arange(V) >> 4)[:, None] + j]
    p[o] = (16 * np.argsort(rng.random((b, C)), axis=0)[:, None, :] + np.argsort(rng.random((b, 16, C)), axis=1)).reshape(V, C)
    al = rng.random(C) < 0.5; p = np.where(al[None, :], p, orders(rng))
    fa[0] = np.where(al, 1, fa[0]); ic[0] = np.where(al, 16 * rng.integers(1, b, C), ic[0])
    return pack(rng, v, cd, p, fa, ic, t)
def setup_inputs_ends(rng):
    v = scores(rng); cd = parents(rng); p = orders(rng); fa, ic, t = moves(rng)
    v[..., 0] = 255 * rng.integers(0, 2, v.shape[:-1]); v[..., W - 1] = 255 * rng.integers(0, 2, v.shape[:-1])
    v[:, :, :, 0] = 0; v[:, :, :, 15] = 255
    o = rng.permutation(V); n = V // 8; me = np.arange(V)[:, None]
    cd[o[:n]] = me[o[:n]]; cd[o[n:2 * n]] = cd[o[n:2 * n], :1]; cd[o[2 * n:3 * n]] = rng.choice(np.array([0, V - 1]), (n, NB)); cd[o[3 * n:4 * n], NB - 1] = o[3 * n:4 * n]
    cd[o[3 * n:], 0] = int(rng.integers(0, V))
    u = rng.integers(0, 4, C)[None, :]
    p = np.where(u == 0, me, np.where(u == 1, V - 1 - me, np.where(u == 2, (me + rng.integers(0, V, C)[None, :]) & (V - 1), p)))
    fa = np.where(rng.random((RO, C)) < 0.5, rng.choice(np.array([1, V - 1]), (RO, C)), fa); ic = np.where(rng.random((RO, C)) < 0.5, rng.choice(np.array([0, 1, V - 1]), (RO, C)), ic)
    return pack(rng, v, cd, p, fa, ic, t)
def setup_inputs_lone(rng):
    v = scores(rng); k = int(rng.integers(0, N)); c = 255 * rng.integers(0, 2, N)
    for r in range(N):
        if r != k: v[r] = c[r]
    p = orders(rng)[:, :3][:, rng.integers(0, 3, C)]; fa, ic, t = moves(rng)
    u = rng.integers(0, 2, (RO, C)); fa = np.take_along_axis(fa[:, :2], u, 1); ic = np.take_along_axis(ic[:, :2], u, 1)
    d = pack(rng, v, parents(rng), p, fa, ic, t); h = d["th"]; o = [int(a) * CN for a in rng.permutation(N)]
    for a, i, x in ((o[0], 1, 17), (o[1], 0, 17), (o[1], 1, 0), (o[3], RO - 1, 17)): h[:, i, a:a + CN] = x
    h[:, :, o[2]:o[2] + CN] = np.minimum(h[:, :, o[2]:o[2] + CN], 16)
    return d
def setup_inputs_votes(rng):
    base = rng.permutation(V); cd = np.empty((V, NB), np.int64); pb = np.empty((V, 1), np.int64); pb[base, 0] = np.arange(V)
    for j in range(V): cd[base[j]] = base[np.resize(rng.permutation(max(j, 1)), NB)]
    pop = np.add.reduce((np.arange(W)[None, :] >> np.arange(NB)[:, None]) & 1, axis=0)
    opp = np.concatenate([rng.permutation(12) < 6, rng.permutation(4) < 2])
    a = rng.integers(52, 73, (N, 8, T, 16, 1)); a[:, :, :, ~opp] = 255; a[N - 1] = 255
    up = (np.arange(16) < 12)[:, None] ^ (opp[:, None] & (np.arange(N) < N - 1)[:, None, None, None, None])
    w = (a * pop) // NB; v = (rng.random(a.shape) * (256 - a)).astype(np.int64) + np.where(up, w, a - w)
    u = rng.integers(0, 6, C)[None, :]
    p = np.where(u < 2, pb, np.where(u == 2, V - 1 - pb, np.where(u == 3, (pb + rng.integers(0, V, C)[None, :]) & (V - 1), orders(rng))))
    fa, ic, t = moves(rng); back = rng.random((RO, C)) < 0.6
    fa = np.where(back, V - 1, fa); ic = np.where(back, V - 1, ic)
    t = np.where(rng.random((RO, C)) < 0.7, rng.choice(np.array([4, 5, 12, 13]), (RO, C)), t)
    return pack(rng, v, cd, p, fa, ic, t)
def setup_inputs_spread(rng):
    s = np.exp2(8 * rng.random((N, 8, T, 1, W), dtype=np.float32)) * (rng.random((N, 8, T, 1, W)) > 0.0625)
    v = np.minimum(np.floor(s * rng.random((N, 8, T, 16, W), dtype=np.float32)), 255)
    fa, ic, t = moves(rng); cd = parents(rng)
    return pack(rng, v, cd, full(rng, cd), fa, ic, t)
def check_inputs(d):
    bad = []
    x = np.asarray(d["tab"]).astype(np.float32)
    if not np.all((x >= 0) & (x <= 255) & (x == np.floor(x))): bad.append("whole numbers of tab")
    for k, lo, hi in (("cand", 0, V - 1), ("pos0", 0, V - 1), ("fac", 1, V - 1), ("inc", 0, V - 1), ("th", 0, 17)):
        if np.min(d[k]) < lo or np.max(d[k]) > hi: bad.append("range of " + k)
    if not np.all(np.sort(d["pos0"], axis=1) == np.arange(V)[None, :, None]): bad.append("orders of pos0")
    if not np.all((np.asarray(d["fac"]) & 1) == 1): bad.append("odd numbers of fac")
    for k in ("pos0", "fac", "inc", "th"):
        if np.any(d[k] != d[k][:1]): bad.append("one " + k + " on all ranks")
    return bad
def reference(tab, cand, pos0, fac, inc, th):
    tb = np.ascontiguousarray(tab.astype(np.float32).astype(np.int32).reshape(N, 8, 16, T, W).transpose(0, 1, 3, 2, 4)).reshape(V, 16, W)
    cd = cand.astype(np.int64).reshape(V, NB)
    def score(p):
        before = (p[cd] < p[:, None, :]).astype(np.int64)
        m = np.add.reduce(before << np.arange(NB)[None, :, None], axis=1)
        return np.add.reduce(np.take_along_axis(tb, m[:, None, :], 2).astype(np.int64), axis=0)
    p = pos0[0].astype(np.int64); F = score(p); flags = []
    for k in range(RO):
        q = (fac[0, k].astype(np.int64) * p + inc[0, k]) & (V - 1)
        G = score(q)
        ok = np.add.reduce((G >= F).astype(np.int64), axis=0) >= th[0, k]
        p = np.where(ok, q, p); F = np.where(ok, G, F); flags.append(ok)
    A = np.stack(flags).astype(np.float32)
    return {"yf": np.ascontiguousarray(F.reshape(16, N, CN).transpose(1, 0, 2)).astype(np.float32), "ya": np.ascontiguousarray(A.reshape(RO, N, CN).transpose(1, 0, 2))}

@@ -1,0 +1,399 @@
+from concourse.bass import DstId, RemoteDMATransfer
+from concourse.mybir import AluOpType as A, ActivationFunctionType as AF
+
+N = 4
+P = dict(TPB=2, XV=30, R=4, RG=4, F=1.2, GAM=1.5, SEND=2.6, BC=3.2, ISS=0.4, BW=260.0, HOP=0.1, TABPOS=4, OWNLAST=1,
+         FIX=0.03, BQ=["pq0", "pq1"], BD=["pd0", "pd1"], BE=["pe2", "px"], BM=["pm"], BS=["ps"])
+PH = [-3.74, -3.68, -3.56, -4.0, -2.78, -3.24, -2.17, -1.27, -1.73, 0.77, -1.68, -1.39, 0.24, 0, -1.21, -0.36, -9.78]
+LA = [0.07, 0.09, 0.12, 0.12, 0.12]
+LAM = 0.21
+BF, F32, I32, U16 = "bfloat16", "float32", "int32", "uint16"
+RING = 6
+SCRATCH = {
+    "tb": ("sbuf", [128, 8192], BF), "posi": ("sbuf", [128, 2048], I32),
+    "x0": ("sbuf", [128, 2048], BF), "xt": ("sbuf", [128, 2048], BF),
+    "kk": ("sbuf", [128, RING * 256], BF), "dg": ("sbuf", [128, RING * 256], BF),
+    "qb": ("sbuf", [128, RING * 256], BF), "bits": ("sbuf", [128, RING * 768], BF),
+    "off": ("sbuf", [128, 40 * 64], U16), "gath": ("sbuf", [128, RING * 1024], BF),
+    "part": ("sbuf", [128, 5 * 256], F32), "land": ("sbuf", [128, 5 * 256], F32),
+    "prm": ("sbuf", [128, 128], F32),
+    "pw": ("sbuf", [128, 352], BF), "nn": ("sbuf", [128, 352], BF),
+    "ss": ("sbuf", [128, 352], BF), "ones": ("sbuf", [128, 128], BF), "idb": ("sbuf", [128, 128], BF),
+    "nid": ("sbuf", [128, 128], BF), "idf": ("sbuf", [128, 128], F32), "isel": ("sbuf", [128, 144], BF),
+    "zz": ("sbuf", [128, 432], BF), "sel": ("sbuf", [128, 16], BF),
+    "it": ("sbuf", [128, 16], I32), "it2": ("sbuf", [128, 16], I32), "it3": ("sbuf", [128, 4], I32),
+    "ucol": ("sbuf", [128, 4], F32), "bcol": ("sbuf", [128, 4], F32),
+    "ci": ("sbuf", [128, 352], I32), "cb": ("sbuf", [128, 352], BF),
+    "fi": ("sbuf", [128, 128], I32), "thi": ("sbuf", [128, 128], I32),
+    "fb": ("sbuf", [128, 128], BF), "thb": ("sbuf", [128, 128], BF), "ft": ("sbuf", [128, 144], F32),
+    "cc": ("sbuf", [128, 4, 16, 2], F32), "cj": ("sbuf", [128, 4, 16, 2], I32),
+    "t0": ("sbuf", [128, 4, 16, 2], F32), "t1": ("sbuf", [128, 4, 16, 2], F32), "t2": ("sbuf", [128, 4, 16, 2], F32),
+    "dd": ("sbuf", [128, 4, 16, 2], F32), "mm": ("sbuf", [128, 4, 16, 2], F32),
+    "fa": ("sbuf", [128, 80], F32), "gg": ("sbuf", [128, 64], F32), "h2": ("sbuf", [128, 128], F32),
+    "vb": ("sbuf", [128, 64], F32), "cn": ("sbuf", [128, 64], F32), "rst": ("sbuf", [128, 64], F32),
+    "ys": ("sbuf", [128, 128], F32),
+    "pq0": ("psum", [128, 512], F32), "pq1": ("psum", [128, 512], F32),
+    "pd0": ("psum", [128, 512], F32), "pd1": ("psum", [128, 512], F32), "pe2": ("psum", [128, 512], F32),
+    "pm": ("psum", [128, 512], F32), "ps": ("psum", [128, 512], F32), "px": ("psum", [128, 512], F32),
+}
+SEMAPHORES = (["pe", "dve", "act", "pool", "sent", "out"] + ["ld%d" % i for i in range(10)]
+              + ["ar%d_%d" % (e, b) for e in range(5) for b in range(2)]
+              + ["pr%d_%d" % (e, b) for e in range(1, 4) for b in range(8)])
+QUEUES = ["pe", "dve", "act", "pool", "sync"]
+
+
+def build(P):
+    ops, last_w, readers, cur = [], {}, {}, [-1, 0]
+    cyc, pcy, fix = 0.00083 * P["F"], 0.000417 * P["F"], P["FIX"]
+    TPB = P["TPB"]; W = 16 * TPB; NB = 4 // TPB
+
+    def add(r, eng, dur, fn, rd=(), wr=(), sem=None, far=(), nbytes=0, lat=0.0):
+        i = len(ops); deps = set()
+        rd = [(r, k) for k in rd]; wr = [(r, k) for k in wr] + list(far)
+        for k in rd:
+            if k in last_w: deps.add(last_w[k])
+        for k in wr:
+            if k in last_w: deps.add(last_w[k])
+            deps.update(readers.get(k, ()))
+        for k in rd: readers.setdefault(k, []).append(i)
+        for k in wr: last_w[k] = i; readers[k] = []
+        ops.append(dict(i=i, n=-3 if nbytes else cur[0], k=cur[1], r=r, eng=eng, dur=dur, fn=fn, deps=deps, sem=sem, nbytes=nbytes, lat=lat))
+        cur[1] += 1
+
+    def V(r, n, fn, rd, wr, k=1): add(r, "dve", max(64 * k, n) * cyc + k * fix, fn, rd, wr)
+    def S(r, n, fn, rd, wr, k=1): add(r, "act", max(64 * k, n) * cyc + k * fix, fn, rd, wr)
+    def M(r, n, fn, rd, wr): add(r, "pe", n * pcy, fn, rd, wr)
+    def G(r, n, fn, rd, wr): add(r, "pool", 0.17 + 2 * n * cyc, fn, rd, wr)
+    def L(r, q, sem, nbytes, fn, rd, wr): add(r, q, 0.1, fn, rd, list(wr) + ["q" + q], sem=sem, nbytes=nbytes, lat=1.8)
+
+    CST = 129.0 - 63.5 / 128.0
+
+    def setup(r):
+        loads = [lambda q=q: L(r, "sync", "ld%d" % (1 + q), 262144,
+                               lambda g, T: g.sync.dma_start(T.posi[:, 512 * q:512 * q + 512], T.pos0[:, 512 * q:512 * q + 512]), [], [("posi", q)])
+                 for q in range(4)]
+        tabs = [lambda h=h: L(r, "sync", "ld%d" % (5 + h), 1048576,
+                              lambda g, T: g.sync.dma_start(T.tb[:, 4096 * h:4096 * h + 4096], T.tab[:, 4096 * h:4096 * h + 4096]), [], [("tb", h)])
+                for h in range(2)]
+        L(r, "sync", "ld0", 1408, lambda g, T: g.sync.dma_start(T.ci[0:1, :], T.cand[:]), [], ["ci"])
+        for f in loads[:P["TABPOS"]] + tabs + loads[P["TABPOS"]:]: f()
+        L(r, "act", "ld7", 32768, lambda g, T: g.scalar.dma_start(T.fi[0:64, :], T.fac[:]), [], ["fi0"])
+        L(r, "act", "ld8", 32768, lambda g, T: g.scalar.dma_start(T.fi[64:128, :], T["inc"][:]), [], ["fi1"])
+        L(r, "act", "ld9", 8192, lambda g, T: g.scalar.dma_start(T.thi[0:16, :], T.th[:, 512 * r:512 * r + 512]), [], ["thi"])
+        V(r, 64, lambda g, T: g.vector.memset(T.ones[:], 1.0), [], ["ones"])
+        def pw(g, T):
+            for i in range(11): x = g.scalar.activation(T.pw[:, i:352:11], T.ones[:, 0:32], AF.Identity, scale=float(2 ** i))
+            return x
+        S(r, 0, pw, ["ones"], ["pw"], 11)
+        V(r, 72, lambda g, T: g.vector.memset(T.isel[:], 0.0), [], ["isel"])
+        G(r, 16, lambda g, T: g.iota(T.it[:], [[-1, 16]], 128, 1), [], ["it"])
+        G(r, 128, lambda g, T: g.affine_select(T.idb[:], T.ones[:], [[-1, 128]], A.is_equal, 0.0, 0, 1), ["ones"], ["idb"])
+        G(r, 352, lambda g, T: g.affine_select(T.pw[:], T.pw[:], [[1, 352]], A.is_ge, 0.0, 352 * r, -11), ["pw"], ["pw"])
+        G(r, 352, lambda g, T: g.affine_select(T.pw[:], T.pw[:], [[-1, 352]], A.is_ge, 0.0, 10 - 352 * r, 11), ["pw"], ["pw"])
+        G(r, 64, lambda g, T: g.affine_select(T.isel[:, 1:128:2], T.ones[:, 0:64], [[-4, 8], [-1000, 2], [-1, 4]],
+                                              A.is_equal, 0.0, 1000 - 32 * r, 1), ["ones", "isel"], ["isel"])
+        V(r, 64, lambda g, T: g.vector.tensor_scalar(T.ucol[:, 0:1], T.it[:, 0:1], -128.0, None, A.add), ["it"], ["ucol"])
+        V(r, 64, lambda g, T: g.vector.tensor_scalar(T.it2[:], T.it[:], 15, None, A.bitwise_and), ["it"], ["it2"])
+        V(r, 64, lambda g, T: g.vector.tensor_scalar(T.sel[:], T.it2[:], 0.0, None, A.is_equal), ["it2"], ["sel"])
+        V(r, 64, lambda g, T: g.vector.tensor_scalar(T.it3[:, 0:1], T.it[:, 0:1], 1, 3, A.logical_shift_right, A.bitwise_and), ["it"], ["it3"])
+        V(r, 64, lambda g, T: g.vector.tensor_scalar(T.bcol[:, 0:1], T.it3[:, 0:1], 2048.0, 1023.5, A.mult, A.add), ["it3"], ["bcol"])
+        S(r, 128, lambda g, T: g.scalar.activation(T.nid[:], T.idb[:], AF.Identity, scale=-1.0), ["idb"], ["nid"])
+        S(r, 128, lambda g, T: g.scalar.activation(T.idf[:], T.idb[:], AF.Copy), ["idb"], ["idf"])
+        S(r, 352, lambda g, T: g.scalar.activation(T.nn[:], T.pw[:], AF.Sign), ["pw"], ["nn"])
+        V(r, 352, lambda g, T: g.vector.tensor_copy(T.cb[0:1, :], T.ci[0:1, :]), ["ci"], ["cb"])
+        M(r, 352, lambda g, T: g.tensor.matmul(T.px[:, 0:352], T.ones[0:1, :], T.cb[0:1, :], True, True), ["ones", "cb"], ["px"])
+        V(r, 352, lambda g, T: g.vector.tensor_scalar(T.px[:, 0:352], T.px[:, 0:352], T.ucol[:, 0:1], None, A.is_equal), ["ucol"], ["px"])
+        V(r, 352, lambda g, T: g.vector.tensor_tensor(T.ss[:], T.nn[:], T.px[:, 0:352], A.subtract), ["nn"], ["px", "ss"])
+        def zmm(g, T):
+            g.tensor.matmul(T.pm[:, 0:144], T.pw[:, 0:128], T.isel[:], True, True)
+            g.tensor.matmul(T.pm[:, 144:288], T.pw[:, 128:256], T.isel[:], True, True)
+            return g.tensor.matmul(T.pm[0:96, 288:432], T.pw[:, 256:352], T.isel[:], True, True)
+        M(r, 432, zmm, ["pw", "isel"], ["pm"])
+        S(r, 288, lambda g, T: g.scalar.activation(T.zz[:, 0:288], T.pm[:, 0:288], AF.Identity, scale=0.5), [], ["pm", "z0"])
+        S(r, 144, lambda g, T: g.scalar.activation(T.zz[0:96, 288:432], T.pm[0:96, 288:432], AF.Copy), [], ["pm", "z2"])
+        V(r, 128, lambda g, T: g.vector.tensor_copy(T.fb[:], T.fi[:]), ["fi0", "fi1"], ["fb"])
+        V(r, 128, lambda g, T: g.vector.tensor_copy(T.thb[0:16, :], T.thi[0:16, :]), ["thi"], ["thb"])
+        def fmm(g, T):
+            g.tensor.matmul(T.ps[:, 0:128], T.fb[:], T.idb[:], True, True)
+            return g.tensor.matmul(T.ps[:, 128:144], T.thb[0:16, :], T.idb[0:16, 0:16], True, True)
+        M(r, 192, fmm, ["fb", "thb", "idb"], ["ps"])
+        S(r, 144, lambda g, T: g.scalar.activation(T.ft[:], T.ps[:, 0:144], AF.Copy), [], ["ps", "ft"])
+        def p0(g, T):
+            g.scalar.activation(T.prm[:, 0:32:2], T.ft[:, 0:16], AF.Identity, scale=1.0 / 128)
+            return g.scalar.activation(T.prm[:, 1:32:2], T.ft[:, 64:80], AF.Identity, scale=1.0 / 128, bias=CST)
+        S(r, 0, p0, ["ft"], [("prm", 0, b) for b in range(4 * NB)], 2)
+        V(r, 128, lambda g, T: g.vector.memset(T.cc[:], 0.0), [], ["cc"])
+        V(r, 64, lambda g, T: g.vector.memset(T.cc[:, :, 0, 1:2], 1.0), [], ["cc"])
+        V(r, 64, lambda g, T: g.vector.memset(T.rst[:], 1.0), [], ["rst"])
+        V(r, 64, lambda g, T: g.vector.memset(T.rst[:, 0:64:16], 0.0), [], ["rst"])
+        V(r, 128, lambda g, T: g.vector.memset(T.dd[:], 0.0), [], [("dd", b) for b in range(NB)] + [("dl", b) for b in range(NB)])
+        def level(k):
+            def f(g, T):
+                for j in range(4):
+                    c = 16 * k + 4 * r + j
+                    x = g.scalar.activation(T.cc[:, j, 2 ** k:2 ** (k + 1), :], T.cc[:, j, 0:2 ** k, :], AF.Identity,
+                                            scale=T.ft[:, c:c + 1], bias=T.ft[:, 64 + c:65 + c])
+                return x
+            S(r, 0, f, ["ft", "cc"], ["cc"], 4)
+        for k in range(3): level(k)
+        V(r, 128, lambda g, T: g.vector.tensor_copy(T.cj[:], T.cc[:]), ["cc"], ["cj"])
+        V(r, 128, lambda g, T: g.vector.tensor_scalar(T.cj[:], T.cj[:], 127, None, A.bitwise_and), ["cj"], ["cj"])
+        V(r, 128, lambda g, T: g.vector.tensor_copy(T.cc[:], T.cj[:]), ["cj"], ["cc"])
+        level(3)
+        def fa2(g, T):
+            g.vector.tensor_tensor(T.cj[:, :, :, 0], T.cc[:, :, :, 1], T.cc[:, :, :, 0], A.subtract)
+            return g.vector.tensor_copy(T.cj[:, :, :, 1], T.cc[:, :, :, 0])
+        V(r, 192, fa2, ["cc"], ["cj"], 2)
+        V(r, 128, lambda g, T: g.vector.tensor_scalar(T.cj[:], T.cj[:], 127, None, A.bitwise_and), ["cj"], ["cj"])
+        def t0(g, T):
+            g.vector.tensor_scalar(T.t0[:, :, :, 0], T.cj[:, :, :, 0], 1.0 / 128, None, A.mult)
+            return g.vector.tensor_scalar(T.t0[:, :, :, 1], T.cj[:, :, :, 1], 1.0 / 128, CST, A.mult, A.add)
+        V(r, 0, t0, ["cj"], [("t", 0, b) for b in range(NB)], 2)
+
+    def unit(r, e, u, n):
+        cur[0] = n; cur[1] = 2 if e == 0 else 0
+        c0 = 256 * u; s = n % P["R"]; sg = n % P["RG"]
+        pq, pd, pe2, pm, ps = [P[x][n % len(P[x])] for x in ("BQ", "BD", "BE", "BM", "BS")]
+        blk = (2 * u) // TPB; own = u // 2
+        if e == 0:
+            V(r, 256, lambda g, T: g.vector.tensor_copy(T.x0[:, c0:c0 + 256], T.posi[:, c0:c0 + 256]), [("posi", u // 2)], [("x0", u)])
+            def xmm(g, T):
+                for j in range(2):
+                    x = g.tensor.matmul(T[pq][:, 128 * j:128 * j + 128], T.x0[:, c0 + 128 * j:c0 + 128 * j + 128], T.idb[:], True, True)
+                return x
+            M(r, 256, xmm, [("x0", u), "idb"], [pq])
+            S(r, 256, lambda g, T: g.scalar.activation(T.xt[:, c0:c0 + 256], T[pq][:, 0:256], AF.Copy), [], [pq, ("xt", u)])
+            qk = ("x0", u); q = lambda T: T.x0[:, c0:c0 + 256]
+        else:
+            for j in range(2):
+                def kd(g, T, j=j):
+                    c = 32 * (e - 1) + 2 * (2 * u + j); a = 256 * s + 128 * j
+                    g.vector.tensor_scalar(T.dg[:, a:a + 128], T.idb[:], T.prm[:, c:c + 1], None, A.mult)
+                    return g.vector.tensor_scalar(T.kk[:, a:a + 128], T.xt[:, c0 + 128 * j:c0 + 128 * j + 128],
+                                                  T.prm[:, c:c + 1], T.prm[:, c + 1:c + 2], A.mult, A.add)
+                V(r, 0, kd, [("xt", u), ("prm", e - 1, blk), "idb"], [("kd", s, j)], 2)
+            for j in range(2):
+                def qmm(g, T, j=j):
+                    a = 256 * s + 128 * j; o = T[pq][:, 128 * j:128 * j + 128]
+                    g.tensor.matmul(o, T.xt[:, c0 + 128 * j:c0 + 128 * j + 128], T.dg[:, a:a + 128], True, False)
+                    return g.tensor.matmul(o, T.kk[:, a:a + 128], T.nid[:], False, True)
+                M(r, 256, qmm, [("kd", s, j), ("xt", u), "nid"], [pq])
+            S(r, 256, lambda g, T: g.scalar.activation(T.qb[:, 256 * s:256 * s + 256], T[pq][:, 0:256], AF.Identity, bias=129.0), [], [pq, ("qb", s)])
+            qk = ("qb", s); q = lambda T: T.qb[:, 256 * s:256 * s + 256]
+        def d01(g, T):
+            g.tensor.matmul(T[pd][:, 0:256], T.ss[:, 0:128], q(T), True, True)
+            return g.tensor.matmul(T[pd][:, 256:512], T.ss[:, 128:256], q(T), True, True)
+        M(r, 512, d01, [qk, "ss"], [pd])
+        M(r, 256, lambda g, T: g.tensor.matmul(T[pe2][0:96, 0:256], T.ss[:, 256:352], q(T), True, True), [qk, "ss"], [pe2])
+        b0 = 768 * s
+        S(r, 512, lambda g, T: g.scalar.activation(T.bits[:, b0:b0 + 512], T[pd][:, 0:512], AF.Sign, bias=-1.0 / 256), [], [pd, ("b0", s)])
+        V(r, 256, lambda g, T: g.vector.tensor_scalar(T.bits[0:96, b0 + 512:b0 + 768], T[pe2][0:96, 0:256], 1.0 / 256, 0.5, A.is_gt, A.subtract), [], [pe2, ("b2", s)])
+        def mk(cs):
+            def f(g, T):
+                for c in cs:
+                    K = 96 if c == 2 else 128
+                    for j in range(2):
+                        for h in range(2):
+                            z = 144 * c + 9 - 8 * h - j; a = b0 + 256 * c + 128 * j
+                            x = g.tensor.matmul(T[pm][:, 0:64], T.zz[0:K, z:z + 128], T.bits[0:K, a + h:a + 128:2],
+                                                c == 2 and j == 0 and h == 0, c == 1 and j == 1 and h == 1)
+                return x
+            return f
+        M(r, 256, mk([2]), [("b2", s), "z2"], [pm])
+        M(r, 512, mk([0, 1]), [("b0", s), "z0"], [pm])
+        o0 = 64 * n; XV = P["XV"]; g0 = 1024 * sg
+        V(r, 64, lambda g, T: g.vector.tensor_scalar(T.off[:, o0:o0 + 64], T[pm][:, 0:64], T.bcol[:, 0:1], None, A.add), ["bcol"], [pm, ("off", n)])
+        tbk = [("off", n), ("tb", 0), ("tb", 1)]
+        V(r, 16 * XV * P["GAM"] + 30, lambda g, T: g.vector.tensor_copy(T.gath[:, g0:g0 + 16 * XV], T.tb[:, 0:8192].indirect(T.off[:, o0:o0 + XV])), tbk, [("gv", sg)])
+        S(r, 16 * (64 - XV) * P["GAM"] + 40, lambda g, T: g.scalar.activation(T.gath[:, g0 + 16 * XV:g0 + 1024], T.tb[:, 0:8192].indirect(T.off[:, o0 + XV:o0 + 64]), AF.Copy), tbk, [("gs", sg)])
+        def sm(g, T):
+            for j in range(2):
+                for t in range(4):
+                    x = g.tensor.matmul(T[ps][:, 16 * j:16 * j + 16], T.gath[:, g0 + 2 * t + j:g0 + 1024:8], T.sel[:], t == 0, t == 3)
+            return x
+        M(r, 512, sm, [("gv", sg), ("gs", sg), "sel"], [ps])
+        lb = blk % NB; w0 = 32 * u - W * blk
+        if own == r:
+            a = 256 * e + 4 * W * lb + 3 * W + w0; f = 32 * (u % 2)
+            if e == 0:
+                S(r, 32, lambda g, T: g.scalar.activation(T.land[:, a:a + 32], T[ps][:, 0:32], AF.Identity, scale=-1.0), [], [ps, ("own", e, u)])
+            elif e == 1:
+                S(r, 32, lambda g, T: g.scalar.activation(T.gg[:, f:f + 32], T[ps][:, 0:32], AF.Copy), [], [ps, ("gg", u)])
+            else:
+                V(r, 32, lambda g, T: g.vector.tensor_tensor(T.land[:, a:a + 32], T.fa[:, f:f + 32], T[ps][:, 0:32], A.subtract), [("F", lb)], [ps, ("own", e, u)])
+        else:
+            a = 256 * e + 32 * u; slot = (r - own - 1) % N
+            S(r, 32, lambda g, T: g.scalar.activation(T.part[:, a:a + 32], T[ps][:, 0:32], AF.Identity, scale=-1.0 if slot == 1 else 1.0), [], [ps, ("part", e, u)])
+            if w0 + 32 == W:
+                src = 256 * e + W * blk; dst = 256 * e + 4 * W * lb + W * slot
+                sem = "ar%d_%d" % (e, lb)
+                def send(g, T, topo):
+                    me, to = T.cores[r], T.cores[own]; rid, pid, _ = topo.addr(to)
+                    return g.remote_dma(T.land[:, dst:dst + W], T.part[:, src:src + W], T.sem[sem], T.sem.sent, pid, rid, topo.mask(me, to))
+                add(r, "pool", P["ISS"], send, [("part", e, x) for x in range(u + 1 - TPB // 2, u + 1)], [],
+                    sem=sem, far=[(own, ("land", e, lb, slot))], lat=P["SEND"])
+
+    def decide(r, e, lb):
+        cur[0] = -2
+        a = 256 * e + 4 * W * lb; j0, j1 = TPB * lb, TPB * lb + TPB; f0 = W * lb; k = e - 1
+        us = range(2 * r + j0 // 2, 2 * r + j1 // 2)
+        if e == 1:
+            V(r, 2 * W, lambda g, T: g.vector.tensor_tensor(T.land[:, a + 3 * W:a + 4 * W], T.fa[:, f0:f0 + W], T.gg[:, f0:f0 + W], A.subtract),
+              [("F", lb)] + [("gg", x) for x in us], [("own", e, x) for x in us])
+        V(r, 4 * W, lambda g, T: g.vector.tensor_tensor(T.h2[:, 0:2 * W], T.land[:, a:a + 2 * W], T.land[:, a + 2 * W:a + 4 * W], A.add),
+          [("land", e, lb, x) for x in range(3)] + [("own", e, x) for x in us], ["h2"])
+        if e == 0:
+            V(r, 2 * W, lambda g, T: g.vector.tensor_tensor(T.fa[:, f0:f0 + W], T.h2[:, 0:W], T.h2[:, W:2 * W], A.subtract), ["h2"], [("F", lb)])
+            return
+        V(r, 2 * W, lambda g, T: g.vector.tensor_tensor(T.vb[:, 0:W], T.h2[:, 0:W], T.h2[:, W:2 * W], A.is_ge), ["h2"], ["vb"])
+        V(r, 2 * W, lambda g, T: g.vector.tensor_tensor(T.dd[:, j0:j1, 8:16, :], T.h2[:, 0:W], T.h2[:, W:2 * W], A.subtract), ["h2"], [("dl", lb)])
+        V(r, W, lambda g, T: g.vector.tensor_tensor_scan(T.cn[:, 0:W], T.rst[:, 0:W], T.vb[:, 0:W], 0.0, A.mult, A.add), ["vb", "rst"], ["cn"])
+        ac = 64 + 4 * k
+        V(r, 64, lambda g, T: g.vector.tensor_tensor(T.fa[:, ac + j0:ac + j1], T.cn[:, 15:W:16], T.ft[:, 128 + 4 * k + j0:128 + 4 * k + j1], A.is_ge),
+          ["cn", "ft"], [("acc", k, lb)])
+        n = 2 ** (3 - k); t = "t%d" % k
+        if k < 3:
+            V(r, 4 * n * TPB, lambda g, T: g.vector.tensor_tensor(T.dd[:, j0:j1, 1:n, :], T[t][:, j0:j1, 3:2 * n:2, :], T[t][:, j0:j1, 2:2 * n:2, :], A.subtract),
+              [("t", k, lb)], [("dd", lb)])
+        def mul(g, T):
+            for j in range(j0, j1):
+                x = g.vector.tensor_scalar(T.mm[:, j, :, :], T.dd[:, j, :, :], T.fa[:, ac + j:ac + j + 1], None, A.mult)
+            return x
+        V(r, 0, mul, [("dd", lb), ("dl", lb), ("acc", k, lb)], [("mm", lb)], TPB)
+        if k < 3:
+            blk = NB * r + lb; c = 32 * e + 2 * TPB * blk; sem = "pr%d_%d" % (e, blk)
+            V(r, 64, lambda g, T: g.vector.tensor_tensor(T.prm[:, c:c + 2 * TPB], T[t][:, j0:j1, 2, :], T.mm[:, j0:j1, 1, :], A.add),
+              [("t", k, lb), ("mm", lb)], [("prm", e, blk)])
+            def cast(g, T, topo):
+                me = T.cores[r]; to = [T.cores[(r + x) % N] for x in range(1, N)]; m = -1
+                for x in to: m &= topo.mask(me, x)
+                ids = [DstId(rid=topo.addr(x)[0], pnc=topo.addr(x)[1]) for x in to]
+                ap = T.prm[:, c:c + 2 * TPB]
+                return g.remote_dma_fused([RemoteDMATransfer(dst_ids=ids, dma_engine_mask=m, remote_sem=T.sem[sem],
+                                                             srcs=[ap], dsts=[ap, ap, ap])], local_sem=T.sem.sent)
+            add(r, "pool", P["ISS"], cast, [("prm", e, blk)], [], sem=sem,
+                far=[((r + x) % N, ("prm", e, blk)) for x in range(1, N)], lat=P["BC"])
+        if k < 2:
+            V(r, 64, lambda g, T: g.vector.tensor_tensor(T["t%d" % (k + 1)][:, j0:j1, 2:n, :], T[t][:, j0:j1, 4:2 * n:2, :], T.mm[:, j0:j1, 2:n, :], A.add),
+              [("t", k, lb), ("mm", lb)], [("t", k + 1, lb)])
+        V(r, 2 * W, lambda g, T: g.vector.tensor_tensor(T.fa[:, f0:f0 + W], T.fa[:, f0:f0 + W], T.mm[:, j0:j1, 8:16, :], A.add),
+          [("mm", lb), ("F", lb)], [("F", lb)])
+
+    def finish(r):
+        cur[0] = -2
+        M(r, 512, lambda g, T: g.tensor.matmul(T.px[0:80, 0:128], T.fa[:], T.idf[:], True, True),
+          [("F", b) for b in range(NB)] + [("acc", k, b) for k in range(4) for b in range(NB)] + ["idf"], ["px"])
+        V(r, 128, lambda g, T: g.vector.tensor_copy(T.ys[0:80, :], T.px[0:80, 0:128]), [], ["px", "ys"])
+        for j in range(4):
+            if j % 2 == 0:
+                L(r, "sync", "out", 8192, lambda g, T, j=j: g.sync.dma_start(T.yf[:, 128 * j:128 * j + 128], T.ys[16 * j:16 * j + 16, :]), ["ys"], [])
+            else:
+                L(r, "act", "out", 8192, lambda g, T, j=j: g.scalar.dma_start(T.yf[:, 128 * j:128 * j + 128], T.ys[16 * j:16 * j + 16, :]), ["ys"], [])
+        L(r, "sync", "out", 8192, lambda g, T: g.sync.dma_start(T.ya[:], T.ys[64:80, :]), ["ys"], [])
+
+    def order(r, e):
+        qs = list(range(4))
+        if e == 4 and P["OWNLAST"]: qs = [q for q in qs if q != r] + [r]
+        if TPB == 4: return [2 * q + h for q in qs for h in range(2)]
+        if e == 4 and P["OWNLAST"]: return [2 * q + h for h in range(2) for q in qs[:3]] + [2 * r, 2 * r + 1]
+        return [2 * q + h for h in range(2) for q in qs]
+
+    for r in range(N): setup(r)
+    for es in ([0, 1], [2], [3], [4]):
+        for r in range(N):
+            n = 0 if es[0] == 0 else 8 * es[0]
+            for u in order(r, es[0]):
+                for e in es:
+                    unit(r, e, u, n); n += 1
+        for r in range(N):
+            for lb in range(NB):
+                for e in es: decide(r, e, lb)
+    for r in range(N): finish(r)
+    return ops
+
+
+def in_line(a, b):
+    return a["eng"] == b["eng"] and a["r"] == b["r"] and (a["eng"] in ("pe", "sync") or bool(a["sem"] and b["sem"]))
+
+
+def schedule(ops, P, ph, la, lam):
+    n = len(ops); hop = P["HOP"]; succ = [[] for _ in ops]
+    for o in ops:
+        for d in o["deps"]: succ[d].append((o["i"], in_line(ops[d], o)))
+    qu = [5 * o["r"] + QUEUES.index(o["eng"]) for o in ops]
+    nb = [o["nbytes"] / P["BW"] / 1000 for o in ops]; lvl = [0.0] * n
+    for o in reversed(ops):
+        i = o["i"]
+        lvl[i] = o["dur"] + max([lvl[x] + (nb[i] if f else hop + o["lat"] + nb[i]) for x, f in succ[i]] + [o["lat"]])
+    key = [(-100 + o["n"] if o["n"] < 0 else o["n"] + ph[o["k"]]) - lam * lvl[o["i"]] for o in ops]
+    left = [len(o["deps"]) for o in ops]; ready = [0.0] * n; free = [0.0] * (5 * N); cand = [[] for _ in free]
+    nxt = [1e9] * (5 * N); dma = [0.0] * N; first = [1] * N; seq = []
+    for i in range(n):
+        if not left[i]: cand[qu[i]].append(i); nxt[qu[i]] = 0.0
+    for _ in range(n):
+        t = min(nxt); q = nxt.index(t); c = cand[q]; b = None; lim = t + la[q % 5]
+        for i in c:
+            if ready[i] <= lim and (b is None or key[i] < key[b]): b = i
+        c.remove(b); o = ops[b]; st = max(t, ready[b]); d = o["dur"]; r = q // 5
+        if o["eng"] == "pool" and o["sem"] and first[r]: first[r] = 0; d += 3
+        free[q] = st + d; f = st + d + o["lat"]
+        if nb[b]: f = max(f, dma[r]) + nb[b]; dma[r] = f
+        seq.append(b)
+        nxt[q] = max(free[q], min(ready[x] for x in c)) if c else 1e9
+        for x, fl in succ[b]:
+            ready[x] = max(ready[x], st + d if fl else f + hop); left[x] -= 1
+            if not left[x]:
+                cand[qu[x]].append(x); nxt[qu[x]] = min(nxt[qu[x]], max(free[qu[x]], ready[x]))
+    return seq
+
+
+PLAN = {}
+
+
+def rank_program(g, core, T, topo):
+    r = T.rank_of(core)
+    if r is None:
+        return
+    if not PLAN:
+        PLAN["ops"] = build(P); PLAN["seq"] = schedule(PLAN["ops"], P, PH, LA, LAM)
+    ops, seq = PLAN["ops"], PLAN["seq"]
+    Q = {"pe": g.tensor, "dve": g.vector, "act": g.scalar, "pool": g, "sync": g.sync}
+    mine = [ops[i] for i in seq if ops[i]["r"] == r]
+
+    def engines(o, dst):
+        return len(topo.engines(T.cores[o["r"]], T.cores[dst]))
+    total = {}
+    for i in set(d for o in mine for d in o["deps"] if ops[d]["r"] != r):
+        total[ops[i]["sem"]] = total.get(ops[i]["sem"], 0) + engines(ops[i], r)
+    pos = {o["i"]: k for k, o in enumerate(mine)}
+    know = {q: {} for q in Q}; after = {}; waits = {}; marked = set()
+    for o in mine:
+        kn = know[o["eng"]]; w = []
+        for d in sorted((ops[x] for x in o["deps"]), key=lambda d: (-pos.get(d["i"], -1), d["i"])):
+            if in_line(d, o): continue
+            if d["r"] == r and d["eng"] == "pool" and d["sem"]: continue
+            key = d["sem"] or d["eng"]; val = pos[d["i"]] if not d["sem"] else 0
+            if kn.get(key, -1) >= val: continue
+            w.append(d); kn[key] = val
+            if not d["sem"]:
+                marked.add(d["i"])
+                for k2, v2 in after[d["i"]].items():
+                    if kn.get(k2, -1) < v2: kn[k2] = v2
+        waits[o["i"]] = w; after[o["i"]] = dict(kn)
+    count = {q: 0 for q in Q}; at = {}; sent = 0; outs = 0
+    for o in mine:
+        q = Q[o["eng"]]
+        for d in waits[o["i"]]:
+            if d["r"] != r: q.wait_ge(T.sem[d["sem"]], total[d["sem"]])
+            elif d["sem"]: q.wait_ge(T.sem[d["sem"]], 16)
+            else: q.wait_ge(T.sem[d["eng"]], at[d["i"]])
+        if o["eng"] == "pool" and o["sem"]:
+            o["fn"](g, T, topo); sent += engines(o, (r + 1) % N)
+        elif o["sem"]:
+            o["fn"](g, T).then_inc(T.sem[o["sem"]], 16); outs += 16 * (o["sem"] == "out")
+        else:
+            x = o["fn"](g, T)
+            if o["i"] in marked:
+                x.then_inc(T.sem[o["eng"]], 1); count[o["eng"]] += 1; at[o["i"]] = count[o["eng"]]
+    g.wait_ge(T.sem.sent, sent)
+    g.sync.wait_ge(T.sem.out, outs)

@@ -2,13 +2,16 @@ from concourse.bass import DstId, RemoteDMATransfer
 from concourse.mybir import AluOpType as A, ActivationFunctionType as AF
 
 N = 4
-P = dict(TPB=2, XV=30, R=4, RG=4, F=1.2, GAM=1.5, SEND=2.6, BC=3.2, ISS=0.4, BW=260.0, HOP=0.1, TABPOS=4, OWNLAST=1,
-         FIX=0.03, BQ=["pq0", "pq1"], BD=["pd0", "pd1"], BE=["pe2", "px"], BM=["pm"], BS=["ps"])
-PH = [-3.74, -3.68, -3.56, -4.0, -2.78, -3.24, -2.17, -1.27, -1.73, 0.77, -1.68, -1.39, 0.24, 0, -1.21, -0.36, -9.78]
-LA = [0.07, 0.09, 0.12, 0.12, 0.12]
-LAM = 0.21
+P = dict(TPB=2, XV=30, R=4, RG=4, F=1.15, PC=0.0006, GAM=1.5, SEND=2.0, BC=2.6, ISS=0.4, BW=260.0, HOP=0.1, TABPOS=4, OWNLAST=1,
+         FIX=0.04, BQ=["pq0", "pq1"], BD=["pd0", "pd1"], BE=["pe2", "px"], BM=["pm"], BS=["ps"])
+PH = [[-3.2, -2.1, -4.4, -3.7, -3.0, -3.5, -2.3, -1.3, -2.7, -1.2, -1.4, -1.7, 0.6, 0.5, 1.5, -6.5, -18.1],
+      [-4.0, -3.3, -3.7, -4.1, -2.8, -7.6, -3.0, -0.9, -1.9, -0.7, -1.7, -1.4, 0.3, 0.1, -0.6, -7.4, -13.8],
+      [-3.8, -3.6, -2.7, -3.4, -2.9, -3.8, -3.4, -1.7, -2.4, -1.5, -1.4, -0.9, 0.3, -0.5, -0.2, -6.1, -19.2],
+      [-3.9, -2.9, -2.4, -2.7, -3.6, -3.6, -2.6, -2.6, -1.7, 0.6, -2.7, -0.3, 0.8, -1.3, -2.4, -6.0, -10.7]]
+LA = [0.07, 0.09, 0.09, 0.12, 0.12]
+LAM = 0.17
 BF, F32, I32, U16 = "bfloat16", "float32", "int32", "uint16"
-RING = 6
+RING = 4
 SCRATCH = {
     "tb": ("sbuf", [128, 8192], BF), "posi": ("sbuf", [128, 2048], I32),
     "x0": ("sbuf", [128, 2048], BF), "xt": ("sbuf", [128, 2048], BF),
@@ -44,7 +47,7 @@ QUEUES = ["pe", "dve", "act", "pool", "sync"]
 
 def build(P):
     ops, last_w, readers, cur = [], {}, {}, [-1, 0]
-    cyc, pcy, fix = 0.00083 * P["F"], 0.000417 * P["F"], P["FIX"]
+    cyc, pcy, fix = 0.00083 * P["F"], P["PC"] * P["F"], P["FIX"]
     TPB = P["TPB"]; W = 16 * TPB; NB = 4 // TPB
 
     def add(r, eng, dur, fn, rd=(), wr=(), sem=None, far=(), nbytes=0, lat=0.0):
@@ -325,7 +328,7 @@ def schedule(ops, P, ph, la, lam):
     for o in reversed(ops):
         i = o["i"]
         lvl[i] = o["dur"] + max([lvl[x] + (nb[i] if f else hop + o["lat"] + nb[i]) for x, f in succ[i]] + [o["lat"]])
-    key = [(-100 + o["n"] if o["n"] < 0 else o["n"] + ph[o["k"]]) - lam * lvl[o["i"]] for o in ops]
+    key = [(-100 + o["n"] if o["n"] < 0 else o["n"] + ph[max(0, o["n"] // 8 - 1)][o["k"]]) - lam * lvl[o["i"]] for o in ops]
     left = [len(o["deps"]) for o in ops]; ready = [0.0] * n; free = [0.0] * (5 * N); cand = [[] for _ in free]
     nxt = [1e9] * (5 * N); dma = [0.0] * N; first = [1] * N; seq = []
     for i in range(n):

@@ -2,28 +2,38 @@ from concourse.bass import DstId, RemoteDMATransfer
 from concourse.mybir import AluOpType as A, ActivationFunctionType as AF
 
 N = 4
-P = dict(TPB=2, XV=30, R=4, RG=4, F=1.15, PC=0.0006, GAM=1.5, SEND=2.0, BC=2.6, ISS=0.4, BW=260.0, HOP=0.1, TABPOS=4, OWNLAST=1,
-         FIX=0.04, BQ=["pq0", "pq1"], BD=["pd0", "pd1"], BE=["pe2", "px"], BM=["pm"], BS=["ps"])
-PH = [[-3.2, -2.1, -4.4, -3.7, -3.0, -3.5, -2.3, -1.3, -2.7, -1.2, -1.4, -1.7, 0.6, 0.5, 1.5, -6.5, -18.1],
-      [-4.0, -3.3, -3.7, -4.1, -2.8, -7.6, -3.0, -0.9, -1.9, -0.7, -1.7, -1.4, 0.3, 0.1, -0.6, -7.4, -13.8],
-      [-3.8, -3.6, -2.7, -3.4, -2.9, -3.8, -3.4, -1.7, -2.4, -1.5, -1.4, -0.9, 0.3, -0.5, -0.2, -6.1, -19.2],
-      [-3.9, -2.9, -2.4, -2.7, -3.6, -3.6, -2.6, -2.6, -1.7, 0.6, -2.7, -0.3, 0.8, -1.3, -2.4, -6.0, -10.7]]
-LA = [0.07, 0.09, 0.09, 0.12, 0.12]
-LAM = 0.17
-BF, F32, I32, U16 = "bfloat16", "float32", "int32", "uint16"
-RING = 4
+P = dict(X1=[44] * 8, XV=[0, 0, 0, 0, 4], X0=["pool"] * 8, ORD=[0, 1, 2, 3, 4, 5, 6, 7], TABPOS=3, SW=1, OWNL=1, H=0, POS=[(0, 2), (2, 4)], KS=[0, 1, 2, 3], QS=[2, 3],
+         F=1.0, PC=0.0005, GAM=1.56, SEND=1.4, BC=2.0, ISS=0.3, FIRST=3.0, BW=260.0, HOP=0.12, FIX=0.055, PFIX=0.012,
+         LA=0.05, AL=0.15, PA=0.7, PB=1.75, T2=26.0, PS=1.35)
+P["AT"] = dict(fx0=-3, fxm=-4, fxc=-4, fkd=-1, fkq=-1.6, ftr=-1, fkt=-0.6, fmq=-3, fwq=0.5, fof=2.3, ftree=7.8,
+               fgv=2.3, fgs=0, fsm=-12, fpa=-12, fse=-12, fow=-5,
+               eo1=-12, eh2=-12, ef0=-12, evb=-12, ecn=-12, eac=-12, emu=-12, epr=-12, eca=-14, edl=-12, eds=-8, etu=10, efu=11,
+               ekq=-12, etr=-12, ekt=-12, ehm=-12, ehc=-12, ehs=-13,
+               ukq=-2.1, utr=-1.8, ukt=-1.5, uwq=-1, ukd=-1.9, umq=-1.45, umc=-1.0, ut2=-0.5, uof=-0.3, ugv=0, ugs=0, usm=1.5, upa=1.95, use=2.3, uow=3.5,
+               dh2=4.1, dvb=4.3, dcn=4.5, dac=4.75, dmu=4.9, dpr=5.2, dca=5.4, ddl=4.8, dds=4, dtu=10, dfu=9, dgg=1,
+               dkq=5.4, dtr=5.6, dkt=5.9, dhm=6.1, dhc=6.5, dhs=6.8)
+P.update({'OWNL': 2, 'X1': [48, 60, 32, 44, 56, 36, 40, 12], 'AT': {'fx0': -6.5, 'fxm': -32.1, 'fxc': -17.5, 'fkd': 3.7, 'fkq': -4.0, 'ftr': 16.9, 'fkt': -12.5, 'fmq': 3.9, 'fwq': 31.0, 'fof': 5.4, 'ftree': 4.9, 'fgv': -4.3, 'fgs': 18.8, 'fsm': 9.2, 'fpa': -9.2, 'fse': -22.1, 'fow': -10.4, 'eo1': -17.7, 'eh2': -0.6, 'ef0': -11.3, 'evb': -31.3, 'ecn': -14.2, 'eac': -0.8, 'emu': -10.2, 'epr': -13.9, 'eca': -11.7, 'edl': -12.0, 'eds': -21.1, 'etu': -6.3, 'efu': 14.7, 'ukq': -2.1, 'utr': -1.5, 'ukt': -1.4, 'uwq': -38.1, 'ukd': -1.7, 'umq': -4.7, 'umc': -11.6, 'ut2': -21.2, 'uof': -5.0, 'ugv': -31.8, 'ugs': -15.4, 'usm': -8.6, 'upa': 2.9, 'use': 39.2, 'uow': 6.4, 'dh2': -4.9, 'dvb': -10.7, 'dcn': -2.0, 'dac': -57.5, 'dmu': -11.4, 'dpr': -20.9, 'dca': -11.2, 'ddl': 6.3, 'dds': -2.0, 'dtu': 12.8, 'dfu': 12.2, 'dgg': 5.5}, 'LA': 0.03, 'AL': 0.2, 'PA': 0.58, 'PB': 0.95, 'T2': 32.79, 'PS': 1.7})
+P.update({'TABPOS': 2, 'FIRST': 6.0, 'X1': [32, 60, 32, 44, 56, 32, 40, 12], 'AT': {'fx0': -12.8, 'fxm': -53.7, 'fxc': -26.8, 'fkd': 4.2, 'fkq': -6.9, 'ftr': 15.7, 'fkt': 2.3, 'fmq': 12.7, 'fwq': 32.8, 'fof': 5.6, 'ftree': 3.1, 'fgv': -4.3, 'fgs': 18.0, 'fsm': 11.9, 'fpa': -5.5, 'fse': -13.3, 'fow': -17.0, 'eo1': -15.4, 'eh2': -6.1, 'ef0': -5.6, 'evb': -22.5, 'ecn': -17.4, 'eac': -3.1, 'emu': -0.3, 'epr': -19.4, 'eca': -7.6, 'edl': -22.3, 'eds': -21.3, 'etu': -16.9, 'efu': -2.2, 'ukq': -2.8, 'utr': 4.8, 'ukt': -2.3, 'uwq': -26.4, 'ukd': -2.4, 'umq': -12.6, 'umc': -10.9, 'ut2': -16.9, 'uof': -9.0, 'ugv': -36.5, 'ugs': -33.7, 'usm': -12.5, 'upa': 2.3, 'use': 59.7, 'uow': 4.6, 'dh2': -4.7, 'dvb': -3.6, 'dcn': 2.4, 'dac': -78.3, 'dmu': -16.5, 'dpr': -24.3, 'dca': -7.7, 'ddl': 5.7, 'dds': -2.9, 'dtu': 9.3, 'dfu': 12.0, 'dgg': 14.8}, 'LA': 0.03, 'AL': 0.2, 'PA': 0.5, 'PB': 1.14, 'T2': 44.53, 'PS': 1.7})
+P.update(dict(TABPOS=3, FIRST=4., PC=.0007, PFIX=0., FIX=.054, F=1.03, GAM=1.6, BW=240., SEND=1.5, BC=2.1, HOP=.125))
+P.update({'X1': [52, 56, 28, 52, 52, 12, 44, 72, 76, 40, 44, 44, 36, 60, 32, 44, 48, 52, 60, 48, 52, 76, 12, 4, 20, 52, 48, 76, 44, 48, 24, 40], 'AT': {'fx0': -8.4, 'fxm': -9.1, 'fxc': -15.1, 'fkd': 5.3, 'fkq': 3.5, 'ftr': 7.1, 'fkt': -7.3, 'fmq': 10.8, 'fwq': 7.6, 'fof': -4.2, 'ftree': 9.6, 'fgv': 5.7, 'fgs': 1.2, 'fsm': -17.3, 'fpa': -8.1, 'fse': -13.2, 'fow': -16.3, 'eo1': -3.2, 'eh2': -5.5, 'ef0': -17.5, 'evb': -12.2, 'ecn': -13.9, 'eac': -2.2, 'emu': -11.2, 'epr': -13.7, 'eca': -6.0, 'edl': 1.5, 'eds': -15.0, 'etu': -10.8, 'efu': 6.7, 'ukq': -3.1, 'utr': -2.7, 'ukt': -1.6, 'uwq': -22.6, 'ukd': -1.8, 'umq': -1.4, 'umc': -3.9, 'ut2': -10.7, 'uof': -8.2, 'ugv': -10.2, 'ugs': -9.9, 'usm': -4.0, 'upa': 0.8, 'use': 25, 'uow': 12.2, 'dh2': -3.1, 'dvb': -16.6, 'dcn': -6.7, 'dac': -20.7, 'dmu': -10.5, 'dpr': -22.1, 'dca': -2.4, 'ddl': 3.6, 'dds': -0.3, 'dtu': 8.1, 'dfu': 13.3, 'dgg': -3.5}, 'LA': 0.03, 'AL': 0.11, 'PA': 0.18, 'PB': 1.5, 'T2': 27.4, 'PS': 1.6})
+P.update(dict(FIRST=4., PC=.0005, PFIX=0.012, FIX=.057, F=1.04, GAM=1.6, BW=205., SEND=1.5, BC=2.1, HOP=.125,
+              TABPOS=2, X1=[56] * 32, LA=0.05, AL=0.2, KS=[0, 1, 2, 3], QS=[], IT=9))
+P.update(dict(F=1.1, GAM=1.72, FIX=.06, SEND=1.65, BC=2.3, HOP=.135, XV=[0, 0, 0, 0, 4], BW=190., X1=[52] * 32, ORD=[0, 2, 1, 3, 4, 6, 5, 7]))
+EARLY = ("fx0", "fxm", "fxc", "fkd", "fkq", "ftr", "fkt", "fmq", "fwq", "fof", "ftree")
+BF, F16, F32, I32, U16 = "bfloat16", "float16", "float32", "int32", "uint16"
+RING = 8
 SCRATCH = {
-    "tb": ("sbuf", [128, 8192], BF), "posi": ("sbuf", [128, 2048], I32),
-    "x0": ("sbuf", [128, 2048], BF), "xt": ("sbuf", [128, 2048], BF),
-    "kk": ("sbuf", [128, RING * 256], BF), "dg": ("sbuf", [128, RING * 256], BF),
-    "qb": ("sbuf", [128, RING * 256], BF), "bits": ("sbuf", [128, RING * 768], BF),
-    "off": ("sbuf", [128, 40 * 64], U16), "gath": ("sbuf", [128, RING * 1024], BF),
-    "part": ("sbuf", [128, 5 * 256], F32), "land": ("sbuf", [128, 5 * 256], F32),
-    "prm": ("sbuf", [128, 128], F32),
-    "pw": ("sbuf", [128, 352], BF), "nn": ("sbuf", [128, 352], BF),
-    "ss": ("sbuf", [128, 352], BF), "ones": ("sbuf", [128, 128], BF), "idb": ("sbuf", [128, 128], BF),
-    "nid": ("sbuf", [128, 128], BF), "idf": ("sbuf", [128, 128], F32), "isel": ("sbuf", [128, 144], BF),
-    "zz": ("sbuf", [128, 432], BF), "sel": ("sbuf", [128, 16], BF),
+    "tb": ("sbuf", [128, 8192], BF), "posi": ("sbuf", [128, 2048], I32), "x0": ("sbuf", [128, 2048], BF),
+    "xd": ("sbuf", [128, 16, 480], BF), "kd": ("sbuf", [128, RING, 88, 2, 4], F16), "kd4": ("sbuf", [128, 8, 88, 4, 4], F16),
+    "kk": ("sbuf", [128, 2048], BF), "kt": ("sbuf", [128, 2048], BF), "mk": ("sbuf", [128, 4, 17, 8], F16),
+    "off": ("sbuf", [128, 40 * 64], U16), "gath": ("sbuf", [128, 16 * 1024], BF),
+    "part": ("sbuf", [128, 5 * 256], F32), "land": ("sbuf", [128, 5, 5, 64], F32),
+    "prm": ("sbuf", [128, 32], F32), "nx": ("sbuf", [128, 3, 4, 2], F32), "sx": ("sbuf", [128, 3, 8, 4], F32),
+    "hs": ("sbuf", [128, 3, 2, 256], F32), "hl": ("sbuf", [128, 3, 8, 64], F32),
+    "nn": ("sbuf", [128, 352], BF), "ss": ("sbuf", [128, 480], BF), "ones": ("sbuf", [128, 352], BF),
+    "idb": ("sbuf", [128, 128], BF), "idp": ("sbuf", [128, 11 * 128], BF), "idf": ("sbuf", [128, 128], F32),
+    "wl": ("sbuf", [128, 4, 32], F16), "w2": ("sbuf", [128, 32, 12], F16), "w4": ("sbuf", [128, 35, 4], F16),
+    "zero": ("sbuf", [128, 544], BF), "sel": ("sbuf", [128, 16], BF),
     "it": ("sbuf", [128, 16], I32), "it2": ("sbuf", [128, 16], I32), "it3": ("sbuf", [128, 4], I32),
     "ucol": ("sbuf", [128, 4], F32), "bcol": ("sbuf", [128, 4], F32),
     "ci": ("sbuf", [128, 352], I32), "cb": ("sbuf", [128, 352], BF),
@@ -32,25 +42,27 @@ SCRATCH = {
     "cc": ("sbuf", [128, 4, 16, 2], F32), "cj": ("sbuf", [128, 4, 16, 2], I32),
     "t0": ("sbuf", [128, 4, 16, 2], F32), "t1": ("sbuf", [128, 4, 16, 2], F32), "t2": ("sbuf", [128, 4, 16, 2], F32),
     "dd": ("sbuf", [128, 4, 16, 2], F32), "mm": ("sbuf", [128, 4, 16, 2], F32),
-    "fa": ("sbuf", [128, 80], F32), "gg": ("sbuf", [128, 64], F32), "h2": ("sbuf", [128, 128], F32),
+    "fa": ("sbuf", [128, 64], F32), "dl": ("sbuf", [128, 64], F32), "gg": ("sbuf", [128, 64], F32), "ow": ("sbuf", [128, 64], F32),
+    "h2": ("sbuf", [128, 128], F32), "mf": ("sbuf", [128, 128], F32),
     "vb": ("sbuf", [128, 64], F32), "cn": ("sbuf", [128, 64], F32), "rst": ("sbuf", [128, 64], F32),
     "ys": ("sbuf", [128, 128], F32),
-    "pq0": ("psum", [128, 512], F32), "pq1": ("psum", [128, 512], F32),
-    "pd0": ("psum", [128, 512], F32), "pd1": ("psum", [128, 512], F32), "pe2": ("psum", [128, 512], F32),
-    "pm": ("psum", [128, 512], F32), "ps": ("psum", [128, 512], F32), "px": ("psum", [128, 512], F32),
+    "px0": ("psum", [128, 512], F32), "px1": ("psum", [128, 512], F32),
+    "pt0": ("psum", [128, 1024], BF), ("ph" if P["H"] else "pt1"): ("psum", [128, 512], F32) if P["H"] else ("psum", [128, 1024], BF),
+    "pm0": ("psum", [128, 512], F32), "pm1": ("psum", [128, 512], F32),
+    "ps0": ("psum", [128, 512], F32), "ps1": ("psum", [128, 512], F32),
 }
-SEMAPHORES = (["pe", "dve", "act", "pool", "sent", "out"] + ["ld%d" % i for i in range(10)]
-              + ["ar%d_%d" % (e, b) for e in range(5) for b in range(2)]
-              + ["pr%d_%d" % (e, b) for e in range(1, 4) for b in range(8)])
+SEMAPHORES = (["pe", "dve", "act", "pool", "sent", "out", "wx"]  + ["ld%d" % i for i in range(10)]
+              + ["ar0_0", "ar1_0"] + ["ar%d_%d" % (e, b) for e in range(2, 5) for b in range(2)]
+              + ["pr1_%d" % (2 * b) for b in range(4)] + ["pr%d_%d" % (e, b) for e in range(2, 4) for b in range(8)]
+              + ["hq%d_%d" % (e, b) for e in range(1, 4) for b in range(8)])
 QUEUES = ["pe", "dve", "act", "pool", "sync"]
 
 
 def build(P):
-    ops, last_w, readers, cur = [], {}, {}, [-1, 0]
-    cyc, pcy, fix = 0.00083 * P["F"], P["PC"] * P["F"], P["FIX"]
-    TPB = P["TPB"]; W = 16 * TPB; NB = 4 // TPB
+    ops, last_w, readers, cur = [], {}, {}, ["s", 0]
+    cyc, pcy, fix, pfix = 0.00083 * P["F"], P["PC"] * P["F"], P["FIX"], P["PFIX"]
 
-    def add(r, eng, dur, fn, rd=(), wr=(), sem=None, far=(), nbytes=0, lat=0.0):
+    def add(st, r, eng, dur, fn, rd=(), wr=(), sem=None, far=(), nbytes=0, lat=0.0):
         i = len(ops); deps = set()
         rd = [(r, k) for k in rd]; wr = [(r, k) for k in wr] + list(far)
         for k in rd:
@@ -60,76 +72,100 @@ def build(P):
             deps.update(readers.get(k, ()))
         for k in rd: readers.setdefault(k, []).append(i)
         for k in wr: last_w[k] = i; readers[k] = []
-        ops.append(dict(i=i, n=-3 if nbytes else cur[0], k=cur[1], r=r, eng=eng, dur=dur, fn=fn, deps=deps, sem=sem, nbytes=nbytes, lat=lat))
-        cur[1] += 1
+        ops.append(dict(i=i, st=cur[0] + st, n=cur[1], r=r, eng=eng, dur=dur, fn=fn, deps=deps, sem=sem, nbytes=nbytes, lat=lat))
 
-    def V(r, n, fn, rd, wr, k=1): add(r, "dve", max(64 * k, n) * cyc + k * fix, fn, rd, wr)
-    def S(r, n, fn, rd, wr, k=1): add(r, "act", max(64 * k, n) * cyc + k * fix, fn, rd, wr)
-    def M(r, n, fn, rd, wr): add(r, "pe", n * pcy, fn, rd, wr)
-    def G(r, n, fn, rd, wr): add(r, "pool", 0.17 + 2 * n * cyc, fn, rd, wr)
-    def L(r, q, sem, nbytes, fn, rd, wr): add(r, q, 0.1, fn, rd, list(wr) + ["q" + q], sem=sem, nbytes=nbytes, lat=1.8)
+    def V(st, r, n, fn, rd, wr, k=1): add(st, r, "dve", max(64 * k, n) * cyc + k * fix, fn, rd, wr)
+    def S(st, r, n, fn, rd, wr, k=1): add(st, r, "act", max(64 * k, n) * cyc + k * fix, fn, rd, wr)
+    def M(st, r, n, fn, rd, wr, k=1): add(st, r, "pe", n * pcy + k * pfix, fn, rd, wr)
+    def G(st, r, n, fn, rd, wr): add(st, r, "pool", 0.17 + 2 * n * cyc, fn, rd, wr)
+    def L(r, q, sem, nbytes, fn, rd, wr): add("", r, q, 0.1, fn, rd, list(wr) + ["q" + q], sem=sem, nbytes=nbytes, lat=1.8)
+
+    def send(st, r, to, src, dst, sem, rd, far):
+        def f(g, T, topo):
+            rid, pid, _ = topo.addr(T.cores[to])
+            return g.remote_dma(dst(T), src(T), T.sem[sem], T.sem.sent, pid, rid, topo.mask(T.cores[r], T.cores[to]))
+        add(st, r, "pool", P["ISS"], f, rd, [], sem=sem, far=[(to, far)], lat=P["SEND"])
+
+    def cast(st, r, ap, sem, keys):
+        def f(g, T, topo):
+            me = T.cores[r]; to = [T.cores[(r + x) % N] for x in range(1, N)]; m = -1
+            for x in to: m &= topo.mask(me, x)
+            ids = [DstId(rid=topo.addr(x)[0], pnc=topo.addr(x)[1]) for x in to]
+            return g.remote_dma_fused([RemoteDMATransfer(dst_ids=ids, dma_engine_mask=m, remote_sem=T.sem[sem],
+                                                         srcs=[ap(T)], dsts=[ap(T)] * 3)], local_sem=T.sem.sent)
+        add(st, r, "pool", P["ISS"], f, keys, [], sem=sem, far=[((r + x) % N, y) for x in range(1, N) for y in keys], lat=P["BC"])
 
     CST = 129.0 - 63.5 / 128.0
+    CKD = 1536.0 - 64.5 / 128.0
+    CMK = -2047.0 * 1535.0
+    held = {}
 
     def setup(r):
-        loads = [lambda q=q: L(r, "sync", "ld%d" % (1 + q), 262144,
-                               lambda g, T: g.sync.dma_start(T.posi[:, 512 * q:512 * q + 512], T.pos0[:, 512 * q:512 * q + 512]), [], [("posi", q)])
-                 for q in range(4)]
-        tabs = [lambda h=h: L(r, "sync", "ld%d" % (5 + h), 1048576,
-                              lambda g, T: g.sync.dma_start(T.tb[:, 4096 * h:4096 * h + 4096], T.tab[:, 4096 * h:4096 * h + 4096]), [], [("tb", h)])
-                for h in range(2)]
+        cur[:] = ["s", 0]
+        loads = [lambda a=a, b=b: L(r, "sync", "ld%d" % (1 + a), 262144 * (b - a),
+                                    lambda g, T: g.sync.dma_start(T.posi[:, 512 * a:512 * b], T.pos0[:, 512 * a:512 * b]), [], [("posi", q) for q in range(a, b)])
+                 for a, b in P["POS"]]
+        tabs = [lambda: L(r, "sync", "ld5", 2097152, lambda g, T: g.sync.dma_start(T.tb[:], T.tab[:]), [], [("tb", 0), ("tb", 1)])]
         L(r, "sync", "ld0", 1408, lambda g, T: g.sync.dma_start(T.ci[0:1, :], T.cand[:]), [], ["ci"])
-        for f in loads[:P["TABPOS"]] + tabs + loads[P["TABPOS"]:]: f()
         L(r, "act", "ld7", 32768, lambda g, T: g.scalar.dma_start(T.fi[0:64, :], T.fac[:]), [], ["fi0"])
         L(r, "act", "ld8", 32768, lambda g, T: g.scalar.dma_start(T.fi[64:128, :], T["inc"][:]), [], ["fi1"])
-        L(r, "act", "ld9", 8192, lambda g, T: g.scalar.dma_start(T.thi[0:16, :], T.th[:, 512 * r:512 * r + 512]), [], ["thi"])
-        V(r, 64, lambda g, T: g.vector.memset(T.ones[:], 1.0), [], ["ones"])
-        def pw(g, T):
-            for i in range(11): x = g.scalar.activation(T.pw[:, i:352:11], T.ones[:, 0:32], AF.Identity, scale=float(2 ** i))
+        L(r, "sync", "ld9", 8192, lambda g, T: g.sync.dma_start(T.thi[0:16, :], T.th[:, 512 * r:512 * r + 512]), [], ["thi"])
+        for f in loads[:P["TABPOS"]] + tabs + loads[P["TABPOS"]:]: f()
+        V("", r, 176, lambda g, T: g.vector.memset(T.ones[:], 1.0), [], ["ones"])
+        G("", r, 128, lambda g, T: g.affine_select(T.idb[:], T.ones[:, 0:128], [[-1, 128]], A.is_equal, 0.0, 0, 1), ["ones"], ["idb"])
+        G("", r, 16, lambda g, T: g.iota(T.it[:], [[-1, 16]], 128, 1), [], ["it"])
+        G("", r, 352, lambda g, T: g.affine_select(T.nn[:], T.ones[:], [[0, 11], [-1, 32]], A.is_equal, 0.0, -32 * r, 1), ["ones"], ["nn"])
+        V("", r, 64, lambda g, T: g.vector.tensor_scalar(T.ucol[:, 0:1], T.it[:, 0:1], -128.0, None, A.add), ["it"], ["ucol"])
+        V("", r, 64, lambda g, T: g.vector.tensor_scalar(T.it2[:], T.it[:], 15, None, A.bitwise_and), ["it"], ["it2"])
+        V("", r, 64, lambda g, T: g.vector.tensor_scalar(T.sel[:], T.it2[:], 0.0, None, A.is_equal), ["it2"], ["sel"])
+        V("", r, 64, lambda g, T: g.vector.tensor_scalar(T.it3[:, 0:1], T.it[:, 0:1], 3, None, A.bitwise_and), ["it"], ["it3"])
+        V("", r, 64, lambda g, T: g.vector.tensor_scalar(T.bcol[:, 0:1], T.it3[:, 0:1], 2048.0, None, A.mult), ["it3"], ["bcol"])
+        V("", r, 64, lambda g, T: g.vector.tensor_scalar(T.bcol[:, 1:2], T.it3[:, 0:1], 2048.0, CMK, A.mult, A.add), ["it3"], ["bcol1"])
+        V("", r, 128, lambda g, T: g.vector.memset(T.mf[:], 0.0), [], ["mf"])
+        V("", r, 64, lambda g, T: g.vector.memset(T.land[:, 4, 4, :], 0.0), [], ["mf"])
+        def idp(g, T):
+            for i in range(11): x = g.scalar.activation(T.idp[:, 128 * i:128 * i + 128], T.idb[:], AF.Identity, scale=float(2 ** i))
             return x
-        S(r, 0, pw, ["ones"], ["pw"], 11)
-        V(r, 72, lambda g, T: g.vector.memset(T.isel[:], 0.0), [], ["isel"])
-        G(r, 16, lambda g, T: g.iota(T.it[:], [[-1, 16]], 128, 1), [], ["it"])
-        G(r, 128, lambda g, T: g.affine_select(T.idb[:], T.ones[:], [[-1, 128]], A.is_equal, 0.0, 0, 1), ["ones"], ["idb"])
-        G(r, 352, lambda g, T: g.affine_select(T.pw[:], T.pw[:], [[1, 352]], A.is_ge, 0.0, 352 * r, -11), ["pw"], ["pw"])
-        G(r, 352, lambda g, T: g.affine_select(T.pw[:], T.pw[:], [[-1, 352]], A.is_ge, 0.0, 10 - 352 * r, 11), ["pw"], ["pw"])
-        G(r, 64, lambda g, T: g.affine_select(T.isel[:, 1:128:2], T.ones[:, 0:64], [[-4, 8], [-1000, 2], [-1, 4]],
-                                              A.is_equal, 0.0, 1000 - 32 * r, 1), ["ones", "isel"], ["isel"])
-        V(r, 64, lambda g, T: g.vector.tensor_scalar(T.ucol[:, 0:1], T.it[:, 0:1], -128.0, None, A.add), ["it"], ["ucol"])
-        V(r, 64, lambda g, T: g.vector.tensor_scalar(T.it2[:], T.it[:], 15, None, A.bitwise_and), ["it"], ["it2"])
-        V(r, 64, lambda g, T: g.vector.tensor_scalar(T.sel[:], T.it2[:], 0.0, None, A.is_equal), ["it2"], ["sel"])
-        V(r, 64, lambda g, T: g.vector.tensor_scalar(T.it3[:, 0:1], T.it[:, 0:1], 1, 3, A.logical_shift_right, A.bitwise_and), ["it"], ["it3"])
-        V(r, 64, lambda g, T: g.vector.tensor_scalar(T.bcol[:, 0:1], T.it3[:, 0:1], 2048.0, 1023.5, A.mult, A.add), ["it3"], ["bcol"])
-        S(r, 128, lambda g, T: g.scalar.activation(T.nid[:], T.idb[:], AF.Identity, scale=-1.0), ["idb"], ["nid"])
-        S(r, 128, lambda g, T: g.scalar.activation(T.idf[:], T.idb[:], AF.Copy), ["idb"], ["idf"])
-        S(r, 352, lambda g, T: g.scalar.activation(T.nn[:], T.pw[:], AF.Sign), ["pw"], ["nn"])
-        V(r, 352, lambda g, T: g.vector.tensor_copy(T.cb[0:1, :], T.ci[0:1, :]), ["ci"], ["cb"])
-        M(r, 352, lambda g, T: g.tensor.matmul(T.px[:, 0:352], T.ones[0:1, :], T.cb[0:1, :], True, True), ["ones", "cb"], ["px"])
-        V(r, 352, lambda g, T: g.vector.tensor_scalar(T.px[:, 0:352], T.px[:, 0:352], T.ucol[:, 0:1], None, A.is_equal), ["ucol"], ["px"])
-        V(r, 352, lambda g, T: g.vector.tensor_tensor(T.ss[:], T.nn[:], T.px[:, 0:352], A.subtract), ["nn"], ["px", "ss"])
-        def zmm(g, T):
-            g.tensor.matmul(T.pm[:, 0:144], T.pw[:, 0:128], T.isel[:], True, True)
-            g.tensor.matmul(T.pm[:, 144:288], T.pw[:, 128:256], T.isel[:], True, True)
-            return g.tensor.matmul(T.pm[0:96, 288:432], T.pw[:, 256:352], T.isel[:], True, True)
-        M(r, 432, zmm, ["pw", "isel"], ["pm"])
-        S(r, 288, lambda g, T: g.scalar.activation(T.zz[:, 0:288], T.pm[:, 0:288], AF.Identity, scale=0.5), [], ["pm", "z0"])
-        S(r, 144, lambda g, T: g.scalar.activation(T.zz[0:96, 288:432], T.pm[0:96, 288:432], AF.Copy), [], ["pm", "z2"])
-        V(r, 128, lambda g, T: g.vector.tensor_copy(T.fb[:], T.fi[:]), ["fi0", "fi1"], ["fb"])
-        V(r, 128, lambda g, T: g.vector.tensor_copy(T.thb[0:16, :], T.thi[0:16, :]), ["thi"], ["thb"])
+        S("", r, 1408, idp, ["idb"], ["idp"], 11)
+        V("", r, 272, lambda g, T: g.vector.memset(T.zero[:], 0.0), [], ["zero"])
+        V("", r, 192, lambda g, T: g.vector.tensor_copy(T.w2[:], T.zero[:, 0:384]), ["zero"], ["w2"])
+        V("", r, 70, lambda g, T: g.vector.tensor_copy(T.w4[:], T.zero[:, 0:140]), ["zero"], ["w4"])
+        V("", r, 272, lambda g, T: g.vector.tensor_copy(T.mk[:], T.zero[:]), ["zero"], [("mk", x) for x in range(4)])
+        S("", r, 128, lambda g, T: g.scalar.activation(T.ss[:, 352:480], T.idb[:], AF.Copy), ["idb"], ["ssi"])
+        S("", r, 128, lambda g, T: g.scalar.activation(T.idf[:], T.idb[:], AF.Copy), ["idb"], ["idf"])
+        V("", r, 352, lambda g, T: g.vector.tensor_copy(T.cb[0:1, :], T.ci[0:1, :]), ["ci"], ["cb"])
+        def cmm(g, T):
+            for i in range(11): x = g.tensor.matmul(T.pm0[:, 32 * i:32 * i + 32], T.ones[0:1, 0:128], T.cb[0:1, i:352:11], True, True)
+            return x
+        M("", r, 704, cmm, ["ones", "cb"], ["pm0"], 11)
+        V("", r, 352, lambda g, T: g.vector.tensor_scalar(T.pm0[:, 0:352], T.pm0[:, 0:352], T.ucol[:, 0:1], None, A.is_equal), ["ucol"], ["pm0"])
+        V("", r, 352, lambda g, T: g.vector.tensor_tensor(T.ss[:, 0:352], T.nn[:], T.pm0[:, 0:352], A.subtract), ["nn"], ["pm0", "ss"])
+        def wmm(g, T):
+            for i in range(11): x = g.tensor.matmul(T.pm1[:, 0:32], T.idp[:, 128 * i:128 * i + 128], T.ss[:, 32 * i:32 * i + 32], i == 0, i == 10)
+            return x
+        M("", r, 704, wmm, ["idp", "ss"], ["pm1"], 11)
+        def w4(g, T):
+            g.vector.tensor_scalar(T.wl[:, r, :] if P["H"] else T.w2[:, 0:8, 4:8], T.pm1[:, 0:32], -1.0, None, A.mult)
+            return g.vector.tensor_scalar(T.w4[:, 3:35:4, :], T.pm1[:, 0:32], -1.0, None, A.mult)
+        V("", r, 0, w4, [], ["pm1", ("wl", r) if P["H"] else "w2", "w4"], 2)
+        if P["H"]: cast("", r, lambda T: T.wl[:, r, :], "wx", [("wl", r)])
+        V("", r, 128, lambda g, T: g.vector.tensor_copy(T.fb[:], T.fi[:]), ["fi0", "fi1"], ["fb"])
+        V("", r, 128, lambda g, T: g.vector.tensor_copy(T.thb[0:16, :], T.thi[0:16, :]), ["thi"], ["thb"])
         def fmm(g, T):
-            g.tensor.matmul(T.ps[:, 0:128], T.fb[:], T.idb[:], True, True)
-            return g.tensor.matmul(T.ps[:, 128:144], T.thb[0:16, :], T.idb[0:16, 0:16], True, True)
-        M(r, 192, fmm, ["fb", "thb", "idb"], ["ps"])
-        S(r, 144, lambda g, T: g.scalar.activation(T.ft[:], T.ps[:, 0:144], AF.Copy), [], ["ps", "ft"])
+            g.tensor.matmul(T.ps0[:, 0:128], T.fb[:], T.idb[:], True, True)
+            return g.tensor.matmul(T.ps0[:, 128:144], T.thb[0:16, :], T.idb[0:16, 0:16], True, True)
+        M("", r, 192, fmm, ["fb", "thb", "idb"], ["ps0"], 2)
+        S("", r, 144, lambda g, T: g.scalar.activation(T.ft[:], T.ps0[:, 0:144], AF.Copy), [], ["ps0", "ft"])
         def p0(g, T):
             g.scalar.activation(T.prm[:, 0:32:2], T.ft[:, 0:16], AF.Identity, scale=1.0 / 128)
             return g.scalar.activation(T.prm[:, 1:32:2], T.ft[:, 64:80], AF.Identity, scale=1.0 / 128, bias=CST)
-        S(r, 0, p0, ["ft"], [("prm", 0, b) for b in range(4 * NB)], 2)
-        V(r, 128, lambda g, T: g.vector.memset(T.cc[:], 0.0), [], ["cc"])
-        V(r, 64, lambda g, T: g.vector.memset(T.cc[:, :, 0, 1:2], 1.0), [], ["cc"])
-        V(r, 64, lambda g, T: g.vector.memset(T.rst[:], 1.0), [], ["rst"])
-        V(r, 64, lambda g, T: g.vector.memset(T.rst[:, 0:64:16], 0.0), [], ["rst"])
-        V(r, 128, lambda g, T: g.vector.memset(T.dd[:], 0.0), [], [("dd", b) for b in range(NB)] + [("dl", b) for b in range(NB)])
+        S("", r, 0, p0, ["ft"], ["prm"], 2)
+        V("", r, 128, lambda g, T: g.vector.memset(T.cc[:], 0.0), [], ["cc"])
+        V("", r, 64, lambda g, T: g.vector.memset(T.cc[:, :, 0, 1:2], 1.0), [], ["cc"])
+        V("", r, 64, lambda g, T: g.vector.memset(T.rst[:], 1.0), [], ["rst"])
+        V("", r, 64, lambda g, T: g.vector.memset(T.rst[:, 0:64:16], 0.0), [], ["rst"])
+        V("", r, 128, lambda g, T: g.vector.memset(T.dd[:], 0.0), [], [(x, b) for x in ("dd", "dl") for b in range(2)])
+        cur[:] = ["f", 0]
         def level(k):
             def f(g, T):
                 for j in range(4):
@@ -137,156 +173,236 @@ def build(P):
                     x = g.scalar.activation(T.cc[:, j, 2 ** k:2 ** (k + 1), :], T.cc[:, j, 0:2 ** k, :], AF.Identity,
                                             scale=T.ft[:, c:c + 1], bias=T.ft[:, 64 + c:65 + c])
                 return x
-            S(r, 0, f, ["ft", "cc"], ["cc"], 4)
+            S("tree", r, 0, f, ["ft", "cc"], ["cc"], 4)
         for k in range(3): level(k)
-        V(r, 128, lambda g, T: g.vector.tensor_copy(T.cj[:], T.cc[:]), ["cc"], ["cj"])
-        V(r, 128, lambda g, T: g.vector.tensor_scalar(T.cj[:], T.cj[:], 127, None, A.bitwise_and), ["cj"], ["cj"])
-        V(r, 128, lambda g, T: g.vector.tensor_copy(T.cc[:], T.cj[:]), ["cj"], ["cc"])
+        V("tree", r, 128, lambda g, T: g.vector.tensor_copy(T.cj[:], T.cc[:]), ["cc"], ["cj"])
+        V("tree", r, 128, lambda g, T: g.vector.tensor_scalar(T.cj[:], T.cj[:], 127, None, A.bitwise_and), ["cj"], ["cj"])
+        V("tree", r, 128, lambda g, T: g.vector.tensor_copy(T.cc[:], T.cj[:]), ["cj"], ["cc"])
         level(3)
         def fa2(g, T):
             g.vector.tensor_tensor(T.cj[:, :, :, 0], T.cc[:, :, :, 1], T.cc[:, :, :, 0], A.subtract)
             return g.vector.tensor_copy(T.cj[:, :, :, 1], T.cc[:, :, :, 0])
-        V(r, 192, fa2, ["cc"], ["cj"], 2)
-        V(r, 128, lambda g, T: g.vector.tensor_scalar(T.cj[:], T.cj[:], 127, None, A.bitwise_and), ["cj"], ["cj"])
+        V("tree", r, 192, fa2, ["cc"], ["cj"], 2)
+        V("tree", r, 128, lambda g, T: g.vector.tensor_scalar(T.cj[:], T.cj[:], 127, None, A.bitwise_and), ["cj"], ["cj"])
         def t0(g, T):
             g.vector.tensor_scalar(T.t0[:, :, :, 0], T.cj[:, :, :, 0], 1.0 / 128, None, A.mult)
             return g.vector.tensor_scalar(T.t0[:, :, :, 1], T.cj[:, :, :, 1], 1.0 / 128, CST, A.mult, A.add)
-        V(r, 0, t0, ["cj"], [("t", 0, b) for b in range(NB)], 2)
+        V("tree", r, 0, t0, ["cj"], [("t", 0, b) for b in range(2)], 2)
+
+    def quotients(r, tl, move, key, s, k0, pt="pt0"):
+        def kq(g, T):
+            for j in range(2):
+                x = g.vector.tensor_scalar(T.kk[:, 256 * s + 128 * j:256 * s + 128 * j + 128], T.xd[:, tl + j, 352:480],
+                                           move(T, j, 0), move(T, j, 1), A.mult, A.add)
+            return x
+        def ks(g, T):
+            for j in range(2):
+                x = g.scalar.activation(T.kk[:, 256 * s + 128 * j:256 * s + 128 * j + 128], T.xd[:, tl + j, 352:480], AF.Identity,
+                                        scale=move(T, j, 0), bias=move(T, j, 1))
+            return x
+        if key == "prm" and tl // 4 in P["QS"]:
+            S("kq", r, 256, ks, [("xd", tl), ("xd", tl + 1), key], [("kk", s)], 2)
+        else:
+            V("kq", r, 0, kq, [("xd", tl), ("xd", tl + 1), key], [("kk", s)], 2)
+        def tr(g, T):
+            for j in range(2):
+                x = g.tensor.transpose(T[pt][:, k0 + 128 * j:k0 + 128 * j + 128], T.kk[:, 256 * s + 128 * j:256 * s + 128 * j + 128], T.idb[:])
+            return x
+        M("tr", r, 256, tr, [("kk", s), "idb"], [pt], 2)
+
+    def gather(r, o0, w, xv, slots):
+        g0 = 1024 * slots[0]; rd = [("off", o0), ("tb", 0), ("tb", 1)]
+        if xv:
+            V("gv", r, 16 * xv * P["GAM"], lambda g, T: g.vector.tensor_copy(T.gath[:, g0:g0 + 16 * xv], T.tb[:, 0:8192].indirect(T.off[:, o0:o0 + xv])),
+              rd, [("gv", x) for x in slots])
+        S("gs", r, 16 * (w - xv) * P["GAM"] + 12,
+          lambda g, T: g.scalar.activation(T.gath[:, g0 + 16 * xv:g0 + 16 * w], T.tb[:, 0:8192].indirect(T.off[:, o0 + xv:o0 + w]), AF.Copy),
+          rd, [("gs", x) for x in slots])
+        return [(k, x) for k in ("gv", "gs") for x in slots]
+
+    def sums(r, e, n, u, nt, got, g0):
+        ps = "ps%d" % (n % 2); own = u // 2; lb = u % 2; f = 32 * lb; w = 16 * nt
+        def sm(g, T):
+            for j in range(nt):
+                for t in range(4):
+                    x = g.tensor.matmul(T[ps][:, 16 * j:16 * j + 16], T.gath[:, g0 + 4 * j + t:g0 + 512 * nt:4 * nt], T.sel[:], t == 0, t == 3)
+            return x
+        M("sm", r, 256 * nt, sm, got + ["sel"], [ps], 4 * nt)
+        if own != r:
+            src = 256 * e + 32 * u; slot = (r - own - 1) % N
+            V("pa", r, 64, lambda g, T: g.vector.tensor_scalar(T.part[:, src:src + w], T[ps][:, 0:w], -1.0 if slot == 1 else 1.0, None, A.mult), [], [ps, ("part", e, u)])
+            send("se", r, own, lambda T: T.part[:, src:src + w], lambda T: T.land[:, e, slot, f:f + w], "ar%d_%d" % (e, lb), [("part", e, u)], ("land", e, lb, slot))
+        elif e == 0:
+            V("ow", r, 64, lambda g, T: g.vector.tensor_scalar(T.land[:, 0, 3, :], T[ps][:, 0:w], -1.0, None, A.mult), [], [ps, ("own", e, lb)])
+        elif e == 1:
+            V("ow", r, 64, lambda g, T: g.vector.tensor_copy(T.gg[:], T[ps][:, 0:w]), [], [ps, ("gg", 0), ("gg", 1)])
+        elif e < 4:
+            V("ow", r, 64, lambda g, T: g.vector.tensor_tensor(T.land[:, e, 3, f:f + w], T.fa[:, f:f + w], T[ps][:, 0:w], A.subtract), [("F", lb)], [ps, ("own", e, lb)])
+        elif n >= 38:
+            held[r, lb] = (lambda T: T[ps][:, 0:w]), ps
+        else:
+            V("ow", r, 64, lambda g, T: g.vector.tensor_copy(T.ow[:, f:f + w], T[ps][:, 0:w]), [], [ps, ("ow", lb)])
+            held[r, lb] = (lambda T: T.ow[:, f:f + w]), ("ow", lb)
+
+    def first(r, q, e, n):
+        cur[:] = ["f", n]; pm = "pm%d" % (n % 2)
+        if e == 0:
+            for u in (2 * q, 2 * q + 1):
+                c = 256 * u
+                if P["X0"][u] == "dve":
+                    V("x0", r, 256, lambda g, T, c=c: g.vector.tensor_copy(T.x0[:, c:c + 256], T.posi[:, c:c + 256]), [("posi", q)], [("x0", u)])
+                else:
+                    G("x0", r, 256, lambda g, T, c=c: g.affine_select(T.x0[:, c:c + 256], T.posi[:, c:c + 256], [[0, 256]], A.is_ge, 0.0, 0, 0), [("posi", q)], [("x0", u)])
+                for j in range(2):
+                    tl = 2 * u + j; px = "px%d" % j
+                    M("xm", r, 480, lambda g, T, tl=tl, px=px: g.tensor.matmul(T[px][:, 0:480], T.x0[:, 128 * tl:128 * tl + 128], T.ss[:], True, True),
+                      [("x0", u), "ss", "ssi"], [px])
+                    S("xc", r, 480, lambda g, T, tl=tl, px=px: g.scalar.activation(T.xd[:, tl, :], T[px][:, 0:480], AF.Copy), [], [px, ("xd", tl)])
+        else:
+            for h in range(2):
+                c = 8 * q + 4 * h
+                quotients(r, 4 * q + 2 * h, lambda T, j, i, c=c: T.prm[:, c + 2 * j + i:c + 2 * j + i + 1], "prm", 2 * q + h, 256 * h)
+            if q in P["KS"]:
+                S("kt", r, 512, lambda g, T: g.scalar.activation(T.kt[:, 512 * q:512 * q + 512], T.pt0[:, 0:512], AF.Copy), [], ["pt0", ("kt", 2 * q), ("kt", 2 * q + 1)])
+            else:
+                V("kt", r, 256, lambda g, T: g.vector.tensor_copy(T.kt[:, 512 * q:512 * q + 512], T.pt0[:, 0:512]), [], ["pt0", ("kt", 2 * q), ("kt", 2 * q + 1)])
+        for j in range(4):
+            tl = 4 * q + j
+            V("kd", r, 176, lambda g, T, j=j, tl=tl: g.vector.tensor_scalar(
+                T.kd4[:, n, :, j, :], T.xd[:, tl, 0:352], T.prm[:, 2 * tl:2 * tl + 1] if e else 1.0 / 128, CKD, A.mult, A.add),
+              [("xd", tl)] + ["prm"] * e, [("kd4", n, j)])
+        for i0, i1 in ((0, 4), (4, 8), (8, 11)):
+            def mq(g, T, i0=i0, i1=i1):
+                for i in range(i0, i1):
+                    x = g.tensor.matmul(T[pm][:, 0:128], T.kd4[:, n, 8 * i:8 * i + 8, :, :], T.idp[:, 128 * i:128 * i + 128], i == 0, e == 0 and i == 10)
+                return x
+            M("mq", r, 128 * (i1 - i0), mq, [("kd4", n, j) for j in range(4)] + ["idp"], [pm], i1 - i0)
+        if e:
+            def wq(g, T):
+                for j in range(4):
+                    x = g.tensor.matmul(T[pm][:, 0:128], T.w4[:, 3 - j:35 - j, :], T.kt[:, 512 * q + 128 * j:512 * q + 128 * j + 128], False, j == 3)
+                return x
+            M("wq", r, 512, wq, [("kt", 2 * q), ("kt", 2 * q + 1), "w4"], [pm], 4)
+        V("of", r, 128, lambda g, T: g.vector.tensor_scalar(T.off[:, 128 * n:128 * n + 128], T[pm][:, 0:128], T.bcol[:, 1:2], None, A.add),
+          ["bcol1"], [pm, ("off", 128 * n)])
+        sums(r, e, n, 2 * q, 4, gather(r, 128 * n, 128, P["X1"][8 * r + n], [2 * n, 2 * n + 1]), 2048 * n)
 
     def unit(r, e, u, n):
-        cur[0] = n; cur[1] = 2 if e == 0 else 0
-        c0 = 256 * u; s = n % P["R"]; sg = n % P["RG"]
-        pq, pd, pe2, pm, ps = [P[x][n % len(P[x])] for x in ("BQ", "BD", "BE", "BM", "BS")]
-        blk = (2 * u) // TPB; own = u // 2
-        if e == 0:
-            V(r, 256, lambda g, T: g.vector.tensor_copy(T.x0[:, c0:c0 + 256], T.posi[:, c0:c0 + 256]), [("posi", u // 2)], [("x0", u)])
-            def xmm(g, T):
-                for j in range(2):
-                    x = g.tensor.matmul(T[pq][:, 128 * j:128 * j + 128], T.x0[:, c0 + 128 * j:c0 + 128 * j + 128], T.idb[:], True, True)
-                return x
-            M(r, 256, xmm, [("x0", u), "idb"], [pq])
-            S(r, 256, lambda g, T: g.scalar.activation(T.xt[:, c0:c0 + 256], T[pq][:, 0:256], AF.Copy), [], [pq, ("xt", u)])
-            qk = ("x0", u); q = lambda T: T.x0[:, c0:c0 + 256]
+        cur[:] = ["u", n]
+        s = n % RING; z = n % 4; c = 2 * (u % 2) if e == 2 else 0; ub = u - u % 2 if e == 2 else u
+        pm, po = ("pm0", "px0")[n % 2], ("pm1", "px1")[n % 2]
+        if P["H"]:
+            move = lambda T, j, i: T.sx[:, e - 2, ub, c + j:c + j + 1]
         else:
-            for j in range(2):
-                def kd(g, T, j=j):
-                    c = 32 * (e - 1) + 2 * (2 * u + j); a = 256 * s + 128 * j
-                    g.vector.tensor_scalar(T.dg[:, a:a + 128], T.idb[:], T.prm[:, c:c + 1], None, A.mult)
-                    return g.vector.tensor_scalar(T.kk[:, a:a + 128], T.xt[:, c0 + 128 * j:c0 + 128 * j + 128],
-                                                  T.prm[:, c:c + 1], T.prm[:, c + 1:c + 2], A.mult, A.add)
-                V(r, 0, kd, [("xt", u), ("prm", e - 1, blk), "idb"], [("kd", s, j)], 2)
-            for j in range(2):
-                def qmm(g, T, j=j):
-                    a = 256 * s + 128 * j; o = T[pq][:, 128 * j:128 * j + 128]
-                    g.tensor.matmul(o, T.xt[:, c0 + 128 * j:c0 + 128 * j + 128], T.dg[:, a:a + 128], True, False)
-                    return g.tensor.matmul(o, T.kk[:, a:a + 128], T.nid[:], False, True)
-                M(r, 256, qmm, [("kd", s, j), ("xt", u), "nid"], [pq])
-            S(r, 256, lambda g, T: g.scalar.activation(T.qb[:, 256 * s:256 * s + 256], T[pq][:, 0:256], AF.Identity, bias=129.0), [], [pq, ("qb", s)])
-            qk = ("qb", s); q = lambda T: T.qb[:, 256 * s:256 * s + 256]
-        def d01(g, T):
-            g.tensor.matmul(T[pd][:, 0:256], T.ss[:, 0:128], q(T), True, True)
-            return g.tensor.matmul(T[pd][:, 256:512], T.ss[:, 128:256], q(T), True, True)
-        M(r, 512, d01, [qk, "ss"], [pd])
-        M(r, 256, lambda g, T: g.tensor.matmul(T[pe2][0:96, 0:256], T.ss[:, 256:352], q(T), True, True), [qk, "ss"], [pe2])
-        b0 = 768 * s
-        S(r, 512, lambda g, T: g.scalar.activation(T.bits[:, b0:b0 + 512], T[pd][:, 0:512], AF.Sign, bias=-1.0 / 256), [], [pd, ("b0", s)])
-        V(r, 256, lambda g, T: g.vector.tensor_scalar(T.bits[0:96, b0 + 512:b0 + 768], T[pe2][0:96, 0:256], 1.0 / 256, 0.5, A.is_gt, A.subtract), [], [pe2, ("b2", s)])
-        def mk(cs):
-            def f(g, T):
-                for c in cs:
-                    K = 96 if c == 2 else 128
-                    for j in range(2):
-                        for h in range(2):
-                            z = 144 * c + 9 - 8 * h - j; a = b0 + 256 * c + 128 * j
-                            x = g.tensor.matmul(T[pm][:, 0:64], T.zz[0:K, z:z + 128], T.bits[0:K, a + h:a + 128:2],
-                                                c == 2 and j == 0 and h == 0, c == 1 and j == 1 and h == 1)
-                return x
-            return f
-        M(r, 256, mk([2]), [("b2", s), "z2"], [pm])
-        M(r, 512, mk([0, 1]), [("b0", s), "z0"], [pm])
-        o0 = 64 * n; XV = P["XV"]; g0 = 1024 * sg
-        V(r, 64, lambda g, T: g.vector.tensor_scalar(T.off[:, o0:o0 + 64], T[pm][:, 0:64], T.bcol[:, 0:1], None, A.add), ["bcol"], [pm, ("off", n)])
-        tbk = [("off", n), ("tb", 0), ("tb", 1)]
-        V(r, 16 * XV * P["GAM"] + 30, lambda g, T: g.vector.tensor_copy(T.gath[:, g0:g0 + 16 * XV], T.tb[:, 0:8192].indirect(T.off[:, o0:o0 + XV])), tbk, [("gv", sg)])
-        S(r, 16 * (64 - XV) * P["GAM"] + 40, lambda g, T: g.scalar.activation(T.gath[:, g0 + 16 * XV:g0 + 1024], T.tb[:, 0:8192].indirect(T.off[:, o0 + XV:o0 + 64]), AF.Copy), tbk, [("gs", sg)])
-        def sm(g, T):
-            for j in range(2):
-                for t in range(4):
-                    x = g.tensor.matmul(T[ps][:, 16 * j:16 * j + 16], T.gath[:, g0 + 2 * t + j:g0 + 1024:8], T.sel[:], t == 0, t == 3)
+            move = lambda T, j, i: T.sx[:, e - 2, u, 2 * j + i:2 * j + i + 1]; pt = "pt%d" % (n % 2)
+            quotients(r, 2 * u, move, ("sx", e - 1, u), s, 0, pt)
+            V("kt", r, 128, lambda g, T: g.vector.tensor_copy(T.kt[:, 256 * s:256 * s + 256], T[pt][:, 0:256]), [], [pt, ("kt", s)])
+        for j in range(2):
+            V("kd", r, 176, lambda g, T, j=j: g.vector.tensor_scalar(T.kd[:, s, :, j, :], T.xd[:, 2 * u + j, 0:352], move(T, j, 0), CKD, A.mult, A.add),
+              [("xd", 2 * u + j), ("sx", e - 1, u)], [("kd", s, j)])
+        def mq(g, T):
+            for i in range(11):
+                x = g.tensor.matmul(T[pm][:, 0:64], T.idp[:, 128 * i:128 * i + 128], T.kd[:, s, 8 * i:8 * i + 8, :, :], i == 0, bool(P["H"]) and i == 10)
             return x
-        M(r, 512, sm, [("gv", sg), ("gs", sg), "sel"], [ps])
-        lb = blk % NB; w0 = 32 * u - W * blk
-        if own == r:
-            a = 256 * e + 4 * W * lb + 3 * W + w0; f = 32 * (u % 2)
-            if e == 0:
-                S(r, 32, lambda g, T: g.scalar.activation(T.land[:, a:a + 32], T[ps][:, 0:32], AF.Identity, scale=-1.0), [], [ps, ("own", e, u)])
-            elif e == 1:
-                S(r, 32, lambda g, T: g.scalar.activation(T.gg[:, f:f + 32], T[ps][:, 0:32], AF.Copy), [], [ps, ("gg", u)])
-            else:
-                V(r, 32, lambda g, T: g.vector.tensor_tensor(T.land[:, a:a + 32], T.fa[:, f:f + 32], T[ps][:, 0:32], A.subtract), [("F", lb)], [ps, ("own", e, u)])
+        M("mq", r, 704, mq, [("kd", s, 0), ("kd", s, 1), "idp"], [pm], 11)
+        if P["H"]:
+            hq = (lambda T: T.hs[:, e - 2, u % 2, 64 * r:64 * r + 64]) if u // 2 == r else (lambda T: T.hl[:, e - 2, u, :])
+            V("mc", r, 64, lambda g, T: g.vector.tensor_tensor(T.mk[:, z, 1:17:2, :], T[pm][:, 0:64], hq(T), A.add), [("hq", e - 1, u)], [pm, ("mk", z)])
         else:
-            a = 256 * e + 32 * u; slot = (r - own - 1) % N
-            S(r, 32, lambda g, T: g.scalar.activation(T.part[:, a:a + 32], T[ps][:, 0:32], AF.Identity, scale=-1.0 if slot == 1 else 1.0), [], [ps, ("part", e, u)])
-            if w0 + 32 == W:
-                src = 256 * e + W * blk; dst = 256 * e + 4 * W * lb + W * slot
-                sem = "ar%d_%d" % (e, lb)
-                def send(g, T, topo):
-                    me, to = T.cores[r], T.cores[own]; rid, pid, _ = topo.addr(to)
-                    return g.remote_dma(T.land[:, dst:dst + W], T.part[:, src:src + W], T.sem[sem], T.sem.sent, pid, rid, topo.mask(me, to))
-                add(r, "pool", P["ISS"], send, [("part", e, x) for x in range(u + 1 - TPB // 2, u + 1)], [],
-                    sem=sem, far=[(own, ("land", e, lb, slot))], lat=P["SEND"])
+            def wq(g, T):
+                for j in range(2):
+                    x = g.tensor.matmul(T[pm][:, 0:64], T.kt[:, 256 * s + 128 * j:256 * s + 128 * j + 128], T.w2[:, 0:8, 4 - 4 * j:12 - 4 * j], False, j == 1)
+                return x
+            M("wq", r, 128, wq, [("kt", s), "w2"], [pm], 2)
+            V("mc", r, 64, lambda g, T: g.vector.tensor_scalar(T.mk[:, z, 1:17:2, :], T[pm][:, 0:64], CMK, None, A.add), [], [pm, ("mk", z)])
+        def t2(g, T):
+            for h in range(2):
+                x = g.tensor.matmul(T[po][:, 0:64], T.mk[:, z, 1 - h:17 - h, :], T.idb[:, h:128:2], h == 0, h == 1)
+            return x
+        M("t2", r, 128, t2, [("mk", z), "idb"], [po], 2)
+        o0 = 64 * n
+        V("of", r, 64, lambda g, T: g.vector.tensor_scalar(T.off[:, o0:o0 + 64], T[po][:, 0:64], T.bcol[:, 0:1], None, A.add), ["bcol"], [po, ("off", o0)])
+        sums(r, e, n, u, 2, gather(r, o0, 64, P["XV"][e], [n % 16]), 1024 * (n % 16))
 
-    def decide(r, e, lb):
-        cur[0] = -2
-        a = 256 * e + 4 * W * lb; j0, j1 = TPB * lb, TPB * lb + TPB; f0 = W * lb; k = e - 1
-        us = range(2 * r + j0 // 2, 2 * r + j1 // 2)
+    def share(r, e, lb):
+        blk = 2 * r + lb; key = ("hq", e, blk)
+        quotients(r, 2 * blk, lambda T, j, i: T.nx[:, e - 1, 2 * lb + j, i:i + 1], ("nx", e, lb), blk, 0)
+        V("kt", r, 128, lambda g, T: g.vector.tensor_copy(T.kt[:, 256 * blk:256 * blk + 256], T.pt0[:, 0:256]), [], ["pt0", ("kt", blk)])
+        def hm(g, T):
+            for j in range(2):
+                x = g.tensor.matmul(T.ph[:, 0:256], T.kt[:, 256 * blk + 128 * j:256 * blk + 128 * j + 128], T.w2[:, :, 4 - 4 * j:12 - 4 * j], j == 0, j == 1)
+            return x
+        M("hm", r, 512, hm, [("kt", blk), "w2"], ["ph"], 2)
+        V("hc", r, 256, lambda g, T: g.vector.tensor_scalar(T.hs[:, e - 1, lb, :], T.ph[:, 0:256], CMK, None, A.add), [], ["ph", key])
+        for x in range(1, N):
+            to = (r + x) % N
+            send("hs", r, to, lambda T, to=to: T.hs[:, e - 1, lb, 64 * to:64 * to + 64], lambda T: T.hl[:, e - 1, blk, :], "hq%d_%d" % (e, blk), [key], key)
+
+    def decide(r, e, lbs):
+        cur[:] = ["e", 2 * r + e] if e < 2 else ["d", 8 * e + order(r, e).index(2 * r + lbs[0])]
+        k = e - 1; lb = lbs[0]; j0, j1 = 2 * lb, 2 * lbs[-1] + 2; f0, f1 = 16 * j0, 16 * j1; w = f1 - f0; h0 = 2 * f0
+        def ks(*name): return [name + (b,) for b in lbs]
+        landed = [("land", e, lb, x) for x in range(3)]
+        ha, hb = (lambda T: T.h2[:, h0:h0 + w]), (lambda T: T.h2[:, h0 + w:h0 + 2 * w])
         if e == 1:
-            V(r, 2 * W, lambda g, T: g.vector.tensor_tensor(T.land[:, a + 3 * W:a + 4 * W], T.fa[:, f0:f0 + W], T.gg[:, f0:f0 + W], A.subtract),
-              [("F", lb)] + [("gg", x) for x in us], [("own", e, x) for x in us])
-        V(r, 4 * W, lambda g, T: g.vector.tensor_tensor(T.h2[:, 0:2 * W], T.land[:, a:a + 2 * W], T.land[:, a + 2 * W:a + 4 * W], A.add),
-          [("land", e, lb, x) for x in range(3)] + [("own", e, x) for x in us], ["h2"])
+            V("o1", r, 2 * w, lambda g, T: g.vector.tensor_tensor(T.land[:, 1, 3, :], T.fa[:], T.gg[:], A.subtract), ks("F") + ks("gg"), [("own", 1, 0)])
+        V("h2", r, 4 * w, lambda g, T: g.vector.tensor_tensor(T.h2[:, h0:h0 + 2 * w], T.land[:, e, 0:2, f0:f1], T.land[:, e, 2:4, f0:f1], A.add),
+          landed + [("own", e, lb) if e < 4 else ("F", lb)], ks("h2"))
         if e == 0:
-            V(r, 2 * W, lambda g, T: g.vector.tensor_tensor(T.fa[:, f0:f0 + W], T.h2[:, 0:W], T.h2[:, W:2 * W], A.subtract), ["h2"], [("F", lb)])
+            V("f0", r, 2 * w, lambda g, T: g.vector.tensor_tensor(T.fa[:], ha(T), hb(T), A.subtract), ks("h2"), ks("F"))
+            if P["H"]: V("ds", r, 64, lambda g, T: g.vector.tensor_copy(T.w2[:, :, 4:8], T.wl[:]), [("wl", x) for x in range(N)], ["w2"])
             return
-        V(r, 2 * W, lambda g, T: g.vector.tensor_tensor(T.vb[:, 0:W], T.h2[:, 0:W], T.h2[:, W:2 * W], A.is_ge), ["h2"], ["vb"])
-        V(r, 2 * W, lambda g, T: g.vector.tensor_tensor(T.dd[:, j0:j1, 8:16, :], T.h2[:, 0:W], T.h2[:, W:2 * W], A.subtract), ["h2"], [("dl", lb)])
-        V(r, W, lambda g, T: g.vector.tensor_tensor_scan(T.cn[:, 0:W], T.rst[:, 0:W], T.vb[:, 0:W], 0.0, A.mult, A.add), ["vb", "rst"], ["cn"])
-        ac = 64 + 4 * k
-        V(r, 64, lambda g, T: g.vector.tensor_tensor(T.fa[:, ac + j0:ac + j1], T.cn[:, 15:W:16], T.ft[:, 128 + 4 * k + j0:128 + 4 * k + j1], A.is_ge),
-          ["cn", "ft"], [("acc", k, lb)])
+        if e < 4:
+            V("vb", r, 2 * w, lambda g, T: g.vector.tensor_tensor(T.vb[:, f0:f1], ha(T), hb(T), A.is_ge), ks("h2"), ks("vb"))
+            V("dl", r, 2 * w, lambda g, T: g.vector.tensor_tensor(T.dd[:, j0:j1, 8:16, :], ha(T), hb(T), A.subtract), ks("h2"), ks("dl"))
+            acc = lambda T, a, b: T.land[:, 4, 4, 4 * k + a:4 * k + b]
+        else:
+            mine, ps = held[r, lb]
+            V("gg", r, 2 * w, lambda g, T: g.vector.tensor_tensor(T.gg[:, f0:f1], hb(T), ha(T), A.subtract), ks("h2"), ks("gg"))
+            V("vb", r, w, lambda g, T: g.vector.tensor_tensor(T.vb[:, f0:f1], mine(T), T.gg[:, f0:f1], A.is_ge), ks("gg"), [ps] + ks("vb"))
+            V("dl", r, w, lambda g, T: g.vector.tensor_tensor(T.dl[:, f0:f1], mine(T), T.gg[:, f0:f1], A.subtract), ks("gg"), [ps] + ks("dl"))
+            acc = lambda T, a, b: T.mf[:, 76 + a:76 + b]
+        V("cn", r, w, lambda g, T: g.vector.tensor_tensor_scan(T.cn[:, f0:f1], T.rst[:, 0:w], T.vb[:, f0:f1], 0.0, A.mult, A.add), ks("vb") + ["rst"], ks("cn"))
+        V("ac", r, 64, lambda g, T: g.vector.tensor_tensor(acc(T, j0, j1), T.cn[:, f0 + 15:f1:16], T.ft[:, 128 + 4 * k + j0:128 + 4 * k + j1], A.is_ge),
+          ks("cn") + ["ft", "mf"], ks("acc", k))
+        if e == 4:
+            def last(g, T):
+                for j in range(j0, j1):
+                    x = g.vector.tensor_scalar(T.mf[:, 16 * j:16 * j + 16], T.dl[:, 16 * j:16 * j + 16], acc(T, j, j + 1), None, A.mult)
+                return x
+            V("mu", r, 0, last, ks("dl") + ks("acc", k), ks("mm"), j1 - j0)
+            return
         n = 2 ** (3 - k); t = "t%d" % k
-        if k < 3:
-            V(r, 4 * n * TPB, lambda g, T: g.vector.tensor_tensor(T.dd[:, j0:j1, 1:n, :], T[t][:, j0:j1, 3:2 * n:2, :], T[t][:, j0:j1, 2:2 * n:2, :], A.subtract),
-              [("t", k, lb)], [("dd", lb)])
+        V("ds", r, 4 * n * (j1 - j0), lambda g, T: g.vector.tensor_tensor(T.dd[:, j0:j1, 1:n, :], T[t][:, j0:j1, 3:2 * n:2, :], T[t][:, j0:j1, 2:2 * n:2, :], A.subtract),
+          ks("t", k), ks("dd"))
         def mul(g, T):
             for j in range(j0, j1):
-                x = g.vector.tensor_scalar(T.mm[:, j, :, :], T.dd[:, j, :, :], T.fa[:, ac + j:ac + j + 1], None, A.mult)
+                x = g.vector.tensor_scalar(T.mm[:, j, :, :], T.dd[:, j, :, :], acc(T, j, j + 1), None, A.mult)
             return x
-        V(r, 0, mul, [("dd", lb), ("dl", lb), ("acc", k, lb)], [("mm", lb)], TPB)
-        if k < 3:
-            blk = NB * r + lb; c = 32 * e + 2 * TPB * blk; sem = "pr%d_%d" % (e, blk)
-            V(r, 64, lambda g, T: g.vector.tensor_tensor(T.prm[:, c:c + 2 * TPB], T[t][:, j0:j1, 2, :], T.mm[:, j0:j1, 1, :], A.add),
-              [("t", k, lb), ("mm", lb)], [("prm", e, blk)])
-            def cast(g, T, topo):
-                me = T.cores[r]; to = [T.cores[(r + x) % N] for x in range(1, N)]; m = -1
-                for x in to: m &= topo.mask(me, x)
-                ids = [DstId(rid=topo.addr(x)[0], pnc=topo.addr(x)[1]) for x in to]
-                ap = T.prm[:, c:c + 2 * TPB]
-                return g.remote_dma_fused([RemoteDMATransfer(dst_ids=ids, dma_engine_mask=m, remote_sem=T.sem[sem],
-                                                             srcs=[ap], dsts=[ap, ap, ap])], local_sem=T.sem.sent)
-            add(r, "pool", P["ISS"], cast, [("prm", e, blk)], [], sem=sem,
-                far=[((r + x) % N, ("prm", e, blk)) for x in range(1, N)], lat=P["BC"])
+        V("mu", r, 0, mul, ks("dd") + ks("dl") + ks("acc", k), ks("mm"), j1 - j0)
+        made = [("sx", e, 2 * r + b) for b in lbs]
+        if P["H"]:
+            sx = lambda T: T.sx[:, k, 2 * r + lb, 0:j1 - j0]
+            V("pr", r, 64, lambda g, T: g.vector.tensor_tensor(sx(T), T[t][:, j0:j1, 2, 0], T.mm[:, j0:j1, 1, 0], A.add), ks("t", k) + ks("mm"), made)
+            cast("ca", r, sx, "pr%d_%d" % (e, 2 * r + lb), made)
+            V("pr", r, 64, lambda g, T: g.vector.tensor_tensor(T.nx[:, k, j0:j1, :], T[t][:, j0:j1, 2, :], T.mm[:, j0:j1, 1, :], A.add), ks("t", k) + ks("mm"), ks("nx", e))
+            for b in lbs: share(r, e, b)
+        else:
+            sx = lambda T: T.sx[:, k, 2 * r + lb:2 * r + lbs[-1] + 1, :]
+            V("pr", r, 64, lambda g, T: g.vector.tensor_tensor(sx(T), T[t][:, j0:j1, 2, :], T.mm[:, j0:j1, 1, :], A.add), ks("t", k) + ks("mm"), made)
+            cast("ca", r, sx, "pr%d_%d" % (e, 2 * r + lb), made)
         if k < 2:
-            V(r, 64, lambda g, T: g.vector.tensor_tensor(T["t%d" % (k + 1)][:, j0:j1, 2:n, :], T[t][:, j0:j1, 4:2 * n:2, :], T.mm[:, j0:j1, 2:n, :], A.add),
-              [("t", k, lb), ("mm", lb)], [("t", k + 1, lb)])
-        V(r, 2 * W, lambda g, T: g.vector.tensor_tensor(T.fa[:, f0:f0 + W], T.fa[:, f0:f0 + W], T.mm[:, j0:j1, 8:16, :], A.add),
-          [("mm", lb), ("F", lb)], [("F", lb)])
+            V("tu", r, 64, lambda g, T: g.vector.tensor_tensor(T["t%d" % (k + 1)][:, j0:j1, 2:n, :], T[t][:, j0:j1, 4:2 * n:2, :], T.mm[:, j0:j1, 2:n, :], A.add),
+              ks("t", k) + ks("mm"), ks("t", k + 1))
+        V("fu", r, 2 * w, lambda g, T: g.vector.tensor_tensor(T.fa[:, f0:f1] if k < 2 else T.land[:, 4, 3, f0:f1], T.fa[:, f0:f1], T.mm[:, j0:j1, 8:16, :], A.add),
+          ks("mm") + ks("F"), ks("F"))
 
     def finish(r):
-        cur[0] = -2
-        M(r, 512, lambda g, T: g.tensor.matmul(T.px[0:80, 0:128], T.fa[:], T.idf[:], True, True),
-          [("F", b) for b in range(NB)] + [("acc", k, b) for k in range(4) for b in range(NB)] + ["idf"], ["px"])
-        V(r, 128, lambda g, T: g.vector.tensor_copy(T.ys[0:80, :], T.px[0:80, 0:128]), [], ["px", "ys"])
+        cur[:] = ["s", 0]
+        M("", r, 512, lambda g, T: g.tensor.matmul(T.px1[:, 0:128], T.land[:, 4, 3:5, :], T.idf[:], True, False),
+          [("F", b) for b in range(2)] + [("acc", k, b) for k in range(3) for b in range(2)] + ["idf"], ["px1"])
+        M("", r, 512, lambda g, T: g.tensor.matmul(T.px1[:, 0:128], T.mf[:], T.idf[:], False, True), [("mm", b) for b in range(2)], ["px1"])
+        V("", r, 128, lambda g, T: g.vector.tensor_copy(T.ys[0:80, :], T.px1[0:80, 0:128]), [], ["px1", "ys"])
         for j in range(4):
             if j % 2 == 0:
                 L(r, "sync", "out", 8192, lambda g, T, j=j: g.sync.dma_start(T.yf[:, 128 * j:128 * j + 128], T.ys[16 * j:16 * j + 16, :]), ["ys"], [])
@@ -295,22 +411,21 @@ def build(P):
         L(r, "sync", "out", 8192, lambda g, T: g.sync.dma_start(T.ya[:], T.ys[64:80, :]), ["ys"], [])
 
     def order(r, e):
-        qs = list(range(4))
-        if e == 4 and P["OWNLAST"]: qs = [q for q in qs if q != r] + [r]
-        if TPB == 4: return [2 * q + h for q in qs for h in range(2)]
-        if e == 4 and P["OWNLAST"]: return [2 * q + h for h in range(2) for q in qs[:3]] + [2 * r, 2 * r + 1]
-        return [2 * q + h for h in range(2) for q in qs]
+        late = [2 * r, 2 * r + 1][2 - P["OWNL"]:] if e == 4 else []
+        return [u for u in P["ORD"] if u not in late] + late
 
     for r in range(N): setup(r)
-    for es in ([0, 1], [2], [3], [4]):
+    for r in range(N):
+        units = [(q, e) for q in range(N) for e in range(2)]
+        if r == 0 and P["SW"]: units[:3] = [(1, 0), (0, 0), (0, 1)]
+        for n, (q, e) in enumerate(units): first(r, q, e, n)
+    for r in range(N):
+        for e in range(2): decide(r, e, [0, 1])
+    for e in range(2, 5):
         for r in range(N):
-            n = 0 if es[0] == 0 else 8 * es[0]
-            for u in order(r, es[0]):
-                for e in es:
-                    unit(r, e, u, n); n += 1
+            for i, u in enumerate(order(r, e)): unit(r, e, u, 8 * e + i)
         for r in range(N):
-            for lb in range(NB):
-                for e in es: decide(r, e, lb)
+            for lb in range(2): decide(r, e, [lb])
     for r in range(N): finish(r)
     return ops
 
@@ -319,34 +434,68 @@ def in_line(a, b):
     return a["eng"] == b["eng"] and a["r"] == b["r"] and (a["eng"] in ("pe", "sync") or bool(a["sem"] and b["sem"]))
 
 
-def schedule(ops, P, ph, la, lam):
-    n = len(ops); hop = P["HOP"]; succ = [[] for _ in ops]
+def schedule(ops, P):
+    n = len(ops); succ = [[] for _ in ops]; left = [len(o["deps"]) for o in ops]; dur = []
     for o in ops:
-        for d in o["deps"]: succ[d].append((o["i"], in_line(ops[d], o)))
-    qu = [5 * o["r"] + QUEUES.index(o["eng"]) for o in ops]
-    nb = [o["nbytes"] / P["BW"] / 1000 for o in ops]; lvl = [0.0] * n
+        dur.append(max(o["dur"], o["nbytes"] / P["BW"] / 1000) if o["eng"] == "sync" else o["dur"])
+        for d in sorted(o["deps"]):
+            succ[d].append((o["i"], 0.0 if in_line(ops[d], o) else P["HOP"] + ops[d]["lat"]))
+    qu = [5 * o["r"] + QUEUES.index(o["eng"]) for o in ops]; lvl = [0.0] * n; key = [0.0] * n
     for o in reversed(ops):
-        i = o["i"]
-        lvl[i] = o["dur"] + max([lvl[x] + (nb[i] if f else hop + o["lat"] + nb[i]) for x, f in succ[i]] + [o["lat"]])
-    key = [(-100 + o["n"] if o["n"] < 0 else o["n"] + ph[max(0, o["n"] // 8 - 1)][o["k"]]) - lam * lvl[o["i"]] for o in ops]
-    left = [len(o["deps"]) for o in ops]; ready = [0.0] * n; free = [0.0] * (5 * N); cand = [[] for _ in free]
-    nxt = [1e9] * (5 * N); dma = [0.0] * N; first = [1] * N; seq = []
+        i, m, st = o["i"], o["n"], o["st"]
+        lvl[i] = dur[i] + max([lvl[x] + lag for x, lag in succ[i]] + [o["lat"]])
+        if st == "s": key[i] = -100.0 - lvl[i]
+        else: key[i] = P["AT"][st] + (P["PA"] * m if st in EARLY else 10 + P["PB"] * m if m < 8 else P["T2"] + P["PS"] * (m - 16)) + 1e-6 * i
+    ready = [0.0] * n; free = [0.0] * (5 * N); cand = [[] for _ in free]; nxt = [1e9] * (5 * N); seq = []; seen = set()
     for i in range(n):
         if not left[i]: cand[qu[i]].append(i); nxt[qu[i]] = 0.0
     for _ in range(n):
-        t = min(nxt); q = nxt.index(t); c = cand[q]; b = None; lim = t + la[q % 5]
-        for i in c:
-            if ready[i] <= lim and (b is None or key[i] < key[b]): b = i
-        c.remove(b); o = ops[b]; st = max(t, ready[b]); d = o["dur"]; r = q // 5
-        if o["eng"] == "pool" and o["sem"] and first[r]: first[r] = 0; d += 3
-        free[q] = st + d; f = st + d + o["lat"]
-        if nb[b]: f = max(f, dma[r]) + nb[b]; dma[r] = f
-        seq.append(b)
+        t = min(nxt); q = nxt.index(t); c = cand[q]; lim = t + P["LA"]
+        lim += P["AL"] * dur[min((i for i in c if ready[i] <= lim), key=lambda i: key[i])]
+        b = min((i for i in c if ready[i] <= lim), key=lambda i: key[i]); o = ops[b]; d = dur[b]
+        if o["eng"] == "pool" and o["sem"] and o["r"] not in seen: seen.add(o["r"]); d += P["FIRST"]
+        c.remove(b); end = free[q] = max(t, ready[b]) + d; seq.append(b)
         nxt[q] = max(free[q], min(ready[x] for x in c)) if c else 1e9
-        for x, fl in succ[b]:
-            ready[x] = max(ready[x], st + d if fl else f + hop); left[x] -= 1
+        for x, lag in succ[b]:
+            ready[x] = max(ready[x], end + lag); left[x] -= 1
             if not left[x]:
                 cand[qu[x]].append(x); nxt[qu[x]] = min(nxt[qu[x]], max(free[qu[x]], ready[x]))
+    return seq
+
+
+def arrange(ops, P):
+    n = len(ops); succ = [[] for _ in ops]; pred = [[] for _ in ops]; dur = []
+    for o in ops:
+        dur.append(max(o["dur"], o["nbytes"] / P["BW"] / 1000) if o["eng"] == "sync" else o["dur"])
+        for d in sorted(o["deps"]):
+            lag = 0.0 if in_line(ops[d], o) else P["HOP"] + ops[d]["lat"]
+            succ[d].append((o["i"], lag)); pred[o["i"]].append((d, lag))
+    qu = [5 * o["r"] + QUEUES.index(o["eng"]) for o in ops]
+
+    def run(before, after, key, t0, slow):
+        left = [len(x) for x in before]; ready = list(t0); free = [0.0] * (5 * N); cand = [[] for _ in free]
+        nxt = [1e9] * (5 * N); seq = []; end = [0.0] * n; first = {}
+        for i in range(n):
+            if not left[i]: cand[qu[i]].append(i); nxt[qu[i]] = min(nxt[qu[i]], ready[i])
+        for _ in range(n):
+            t = min(nxt); q = nxt.index(t); c = cand[q]; lim = t + P["LA"]
+            lim += P["AL"] * dur[min((i for i in c if ready[i] <= lim), key=lambda i: key[i])]
+            b = min((i for i in c if ready[i] <= lim), key=lambda i: key[i])
+            if slow is None and ops[b]["eng"] == "pool" and ops[b]["sem"]: first.setdefault(q, b)
+            d = dur[b] + P["FIRST"] * (b in slow if slow else first.get(q) == b)
+            c.remove(b); end[b] = free[q] = max(t, ready[b]) + d; seq.append(b)
+            nxt[q] = max(free[q], min(ready[x] for x in c)) if c else 1e9
+            for x, lag in after[b]:
+                ready[x] = max(ready[x], end[b] + lag); left[x] -= 1
+                if not left[x]:
+                    cand[qu[x]].append(x); nxt[qu[x]] = min(nxt[qu[x]], max(free[qu[x]], ready[x]))
+        return seq, end, set(first.values())
+
+    key = [0.0] * n
+    for i in reversed(range(n)): key[i] = min([key[x] - lag for x, lag in succ[i]] + [-ops[i]["lat"]]) - dur[i]
+    for _ in range(P["IT"]):
+        seq, end, slow = run(pred, succ, key, [0.0] * n, None)
+        key = [-x for x in run(succ, pred, [-x for x in end], [o["lat"] for o in ops], slow)[1]]
     return seq
 
 
@@ -358,7 +507,7 @@ def rank_program(g, core, T, topo):
     if r is None:
         return
     if not PLAN:
-        PLAN["ops"] = build(P); PLAN["seq"] = schedule(PLAN["ops"], P, PH, LA, LAM)
+        PLAN["ops"] = build(P); PLAN["seq"] = arrange(PLAN["ops"], P)
     ops, seq = PLAN["ops"], PLAN["seq"]
     Q = {"pe": g.tensor, "dve": g.vector, "act": g.scalar, "pool": g, "sync": g.sync}
     mine = [ops[i] for i in seq if ops[i]["r"] == r]

from concourse.bass import DstId, RemoteDMATransfer
from concourse.mybir import AluOpType as A, ActivationFunctionType as AF

N = 4
P = dict(X1=[44] * 8, XV=[0, 0, 0, 0, 4], X0=["pool"] * 8, ORD=[0, 1, 2, 3, 4, 5, 6, 7], TABPOS=3, SW=1, OWNL=1, H=0, POS=[(0, 2), (2, 4)], KS=[0, 1, 2, 3], QS=[2, 3],
         F=1.0, PC=0.0005, GAM=1.56, SEND=1.4, BC=2.0, ISS=0.3, FIRST=3.0, BW=260.0, HOP=0.12, FIX=0.055, PFIX=0.012,
         LA=0.05, AL=0.15, PA=0.7, PB=1.75, T2=26.0, PS=1.35)
P["AT"] = dict(fx0=-3, fxm=-4, fxc=-4, fkd=-1, fkq=-1.6, ftr=-1, fkt=-0.6, fmq=-3, fwq=0.5, fof=2.3, ftree=7.8,
               fgv=2.3, fgs=0, fsm=-12, fpa=-12, fse=-12, fow=-5,
               eo1=-12, eh2=-12, ef0=-12, evb=-12, ecn=-12, eac=-12, emu=-12, epr=-12, eca=-14, edl=-12, eds=-8, etu=10, efu=11,
               ekq=-12, etr=-12, ekt=-12, ehm=-12, ehc=-12, ehs=-13,
               ukq=-2.1, utr=-1.8, ukt=-1.5, uwq=-1, ukd=-1.9, umq=-1.45, umc=-1.0, ut2=-0.5, uof=-0.3, ugv=0, ugs=0, usm=1.5, upa=1.95, use=2.3, uow=3.5,
               dh2=4.1, dvb=4.3, dcn=4.5, dac=4.75, dmu=4.9, dpr=5.2, dca=5.4, ddl=4.8, dds=4, dtu=10, dfu=9, dgg=1,
               dkq=5.4, dtr=5.6, dkt=5.9, dhm=6.1, dhc=6.5, dhs=6.8)
P.update({'OWNL': 2, 'X1': [48, 60, 32, 44, 56, 36, 40, 12], 'AT': {'fx0': -6.5, 'fxm': -32.1, 'fxc': -17.5, 'fkd': 3.7, 'fkq': -4.0, 'ftr': 16.9, 'fkt': -12.5, 'fmq': 3.9, 'fwq': 31.0, 'fof': 5.4, 'ftree': 4.9, 'fgv': -4.3, 'fgs': 18.8, 'fsm': 9.2, 'fpa': -9.2, 'fse': -22.1, 'fow': -10.4, 'eo1': -17.7, 'eh2': -0.6, 'ef0': -11.3, 'evb': -31.3, 'ecn': -14.2, 'eac': -0.8, 'emu': -10.2, 'epr': -13.9, 'eca': -11.7, 'edl': -12.0, 'eds': -21.1, 'etu': -6.3, 'efu': 14.7, 'ukq': -2.1, 'utr': -1.5, 'ukt': -1.4, 'uwq': -38.1, 'ukd': -1.7, 'umq': -4.7, 'umc': -11.6, 'ut2': -21.2, 'uof': -5.0, 'ugv': -31.8, 'ugs': -15.4, 'usm': -8.6, 'upa': 2.9, 'use': 39.2, 'uow': 6.4, 'dh2': -4.9, 'dvb': -10.7, 'dcn': -2.0, 'dac': -57.5, 'dmu': -11.4, 'dpr': -20.9, 'dca': -11.2, 'ddl': 6.3, 'dds': -2.0, 'dtu': 12.8, 'dfu': 12.2, 'dgg': 5.5}, 'LA': 0.03, 'AL': 0.2, 'PA': 0.58, 'PB': 0.95, 'T2': 32.79, 'PS': 1.7})
P.update({'TABPOS': 2, 'FIRST': 6.0, 'X1': [32, 60, 32, 44, 56, 32, 40, 12], 'AT': {'fx0': -12.8, 'fxm': -53.7, 'fxc': -26.8, 'fkd': 4.2, 'fkq': -6.9, 'ftr': 15.7, 'fkt': 2.3, 'fmq': 12.7, 'fwq': 32.8, 'fof': 5.6, 'ftree': 3.1, 'fgv': -4.3, 'fgs': 18.0, 'fsm': 11.9, 'fpa': -5.5, 'fse': -13.3, 'fow': -17.0, 'eo1': -15.4, 'eh2': -6.1, 'ef0': -5.6, 'evb': -22.5, 'ecn': -17.4, 'eac': -3.1, 'emu': -0.3, 'epr': -19.4, 'eca': -7.6, 'edl': -22.3, 'eds': -21.3, 'etu': -16.9, 'efu': -2.2, 'ukq': -2.8, 'utr': 4.8, 'ukt': -2.3, 'uwq': -26.4, 'ukd': -2.4, 'umq': -12.6, 'umc': -10.9, 'ut2': -16.9, 'uof': -9.0, 'ugv': -36.5, 'ugs': -33.7, 'usm': -12.5, 'upa': 2.3, 'use': 59.7, 'uow': 4.6, 'dh2': -4.7, 'dvb': -3.6, 'dcn': 2.4, 'dac': -78.3, 'dmu': -16.5, 'dpr': -24.3, 'dca': -7.7, 'ddl': 5.7, 'dds': -2.9, 'dtu': 9.3, 'dfu': 12.0, 'dgg': 14.8}, 'LA': 0.03, 'AL': 0.2, 'PA': 0.5, 'PB': 1.14, 'T2': 44.53, 'PS': 1.7})
P.update(dict(TABPOS=3, FIRST=4., PC=.0007, PFIX=0., FIX=.054, F=1.03, GAM=1.6, BW=240., SEND=1.5, BC=2.1, HOP=.125))
P.update({'X1': [52, 56, 28, 52, 52, 12, 44, 72, 76, 40, 44, 44, 36, 60, 32, 44, 48, 52, 60, 48, 52, 76, 12, 4, 20, 52, 48, 76, 44, 48, 24, 40], 'AT': {'fx0': -8.4, 'fxm': -9.1, 'fxc': -15.1, 'fkd': 5.3, 'fkq': 3.5, 'ftr': 7.1, 'fkt': -7.3, 'fmq': 10.8, 'fwq': 7.6, 'fof': -4.2, 'ftree': 9.6, 'fgv': 5.7, 'fgs': 1.2, 'fsm': -17.3, 'fpa': -8.1, 'fse': -13.2, 'fow': -16.3, 'eo1': -3.2, 'eh2': -5.5, 'ef0': -17.5, 'evb': -12.2, 'ecn': -13.9, 'eac': -2.2, 'emu': -11.2, 'epr': -13.7, 'eca': -6.0, 'edl': 1.5, 'eds': -15.0, 'etu': -10.8, 'efu': 6.7, 'ukq': -3.1, 'utr': -2.7, 'ukt': -1.6, 'uwq': -22.6, 'ukd': -1.8, 'umq': -1.4, 'umc': -3.9, 'ut2': -10.7, 'uof': -8.2, 'ugv': -10.2, 'ugs': -9.9, 'usm': -4.0, 'upa': 0.8, 'use': 25, 'uow': 12.2, 'dh2': -3.1, 'dvb': -16.6, 'dcn': -6.7, 'dac': -20.7, 'dmu': -10.5, 'dpr': -22.1, 'dca': -2.4, 'ddl': 3.6, 'dds': -0.3, 'dtu': 8.1, 'dfu': 13.3, 'dgg': -3.5}, 'LA': 0.03, 'AL': 0.11, 'PA': 0.18, 'PB': 1.5, 'T2': 27.4, 'PS': 1.6})
P.update(dict(FIRST=4., PC=.0005, PFIX=0.012, FIX=.057, F=1.04, GAM=1.6, BW=205., SEND=1.5, BC=2.1, HOP=.125,
              TABPOS=2, X1=[56] * 32, LA=0.05, AL=0.2, KS=[0, 1, 2, 3], QS=[], IT=9))
P.update(dict(F=1.1, GAM=1.72, FIX=.06, SEND=1.65, BC=2.3, HOP=.135, XV=[0, 0, 0, 0, 4], BW=190., X1=[52] * 32, ORD=[0, 2, 1, 3, 4, 6, 5, 7]))
EARLY = ("fx0", "fxm", "fxc", "fkd", "fkq", "ftr", "fkt", "fmq", "fwq", "fof", "ftree")
BF, F16, F32, I32, U16 = "bfloat16", "float16", "float32", "int32", "uint16"
RING = 8
SCRATCH = {
    "tb": ("sbuf", [128, 8192], BF), "posi": ("sbuf", [128, 2048], I32), "x0": ("sbuf", [128, 2048], BF),
    "xd": ("sbuf", [128, 16, 480], BF), "kd": ("sbuf", [128, RING, 88, 2, 4], F16), "kd4": ("sbuf", [128, 8, 88, 4, 4], F16),
    "kk": ("sbuf", [128, 2048], BF), "kt": ("sbuf", [128, 2048], BF), "mk": ("sbuf", [128, 4, 17, 8], F16),
    "off": ("sbuf", [128, 40 * 64], U16), "gath": ("sbuf", [128, 16 * 1024], BF),
    "part": ("sbuf", [128, 5 * 256], F32), "land": ("sbuf", [128, 5, 5, 64], F32),
    "prm": ("sbuf", [128, 32], F32), "nx": ("sbuf", [128, 3, 4, 2], F32), "sx": ("sbuf", [128, 3, 8, 4], F32),
    "hs": ("sbuf", [128, 3, 2, 256], F32), "hl": ("sbuf", [128, 3, 8, 64], F32),
    "nn": ("sbuf", [128, 352], BF), "ss": ("sbuf", [128, 480], BF), "ones": ("sbuf", [128, 352], BF),
    "idb": ("sbuf", [128, 128], BF), "idp": ("sbuf", [128, 11 * 128], BF), "idf": ("sbuf", [128, 128], F32),
    "wl": ("sbuf", [128, 4, 32], F16), "w2": ("sbuf", [128, 32, 12], F16), "w4": ("sbuf", [128, 35, 4], F16),
    "zero": ("sbuf", [128, 544], BF), "sel": ("sbuf", [128, 16], BF),
    "it": ("sbuf", [128, 16], I32), "it2": ("sbuf", [128, 16], I32), "it3": ("sbuf", [128, 4], I32),
    "ucol": ("sbuf", [128, 4], F32), "bcol": ("sbuf", [128, 4], F32),
    "ci": ("sbuf", [128, 352], I32), "cb": ("sbuf", [128, 352], BF),
    "fi": ("sbuf", [128, 128], I32), "thi": ("sbuf", [128, 128], I32),
    "fb": ("sbuf", [128, 128], BF), "thb": ("sbuf", [128, 128], BF), "ft": ("sbuf", [128, 144], F32),
    "cc": ("sbuf", [128, 4, 16, 2], F32), "cj": ("sbuf", [128, 4, 16, 2], I32),
    "t0": ("sbuf", [128, 4, 16, 2], F32), "t1": ("sbuf", [128, 4, 16, 2], F32), "t2": ("sbuf", [128, 4, 16, 2], F32),
    "dd": ("sbuf", [128, 4, 16, 2], F32), "mm": ("sbuf", [128, 4, 16, 2], F32),
    "fa": ("sbuf", [128, 64], F32), "dl": ("sbuf", [128, 64], F32), "gg": ("sbuf", [128, 64], F32), "ow": ("sbuf", [128, 64], F32),
    "h2": ("sbuf", [128, 128], F32), "mf": ("sbuf", [128, 128], F32),
    "vb": ("sbuf", [128, 64], F32), "cn": ("sbuf", [128, 64], F32), "rst": ("sbuf", [128, 64], F32),
    "ys": ("sbuf", [128, 128], F32),
    "px0": ("psum", [128, 512], F32), "px1": ("psum", [128, 512], F32),
    "pt0": ("psum", [128, 1024], BF), ("ph" if P["H"] else "pt1"): ("psum", [128, 512], F32) if P["H"] else ("psum", [128, 1024], BF),
    "pm0": ("psum", [128, 512], F32), "pm1": ("psum", [128, 512], F32),
    "ps0": ("psum", [128, 512], F32), "ps1": ("psum", [128, 512], F32),
}
SEMAPHORES = (["pe", "dve", "act", "pool", "sent", "out", "wx"]  + ["ld%d" % i for i in range(10)]
              + ["ar0_0", "ar1_0"] + ["ar%d_%d" % (e, b) for e in range(2, 5) for b in range(2)]
              + ["pr1_%d" % (2 * b) for b in range(4)] + ["pr%d_%d" % (e, b) for e in range(2, 4) for b in range(8)]
              + ["hq%d_%d" % (e, b) for e in range(1, 4) for b in range(8)])
QUEUES = ["pe", "dve", "act", "pool", "sync"]


def build(P):
    ops, last_w, readers, cur = [], {}, {}, ["s", 0]
    cyc, pcy, fix, pfix = 0.00083 * P["F"], P["PC"] * P["F"], P["FIX"], P["PFIX"]

    def add(st, r, eng, dur, fn, rd=(), wr=(), sem=None, far=(), nbytes=0, lat=0.0):
        i = len(ops); deps = set()
        rd = [(r, k) for k in rd]; wr = [(r, k) for k in wr] + list(far)
        for k in rd:
            if k in last_w: deps.add(last_w[k])
        for k in wr:
            if k in last_w: deps.add(last_w[k])
            deps.update(readers.get(k, ()))
        for k in rd: readers.setdefault(k, []).append(i)
        for k in wr: last_w[k] = i; readers[k] = []
        ops.append(dict(i=i, st=cur[0] + st, n=cur[1], r=r, eng=eng, dur=dur, fn=fn, deps=deps, sem=sem, nbytes=nbytes, lat=lat))

    def V(st, r, n, fn, rd, wr, k=1): add(st, r, "dve", max(64 * k, n) * cyc + k * fix, fn, rd, wr)
    def S(st, r, n, fn, rd, wr, k=1): add(st, r, "act", max(64 * k, n) * cyc + k * fix, fn, rd, wr)
    def M(st, r, n, fn, rd, wr, k=1): add(st, r, "pe", n * pcy + k * pfix, fn, rd, wr)
    def G(st, r, n, fn, rd, wr): add(st, r, "pool", 0.17 + 2 * n * cyc, fn, rd, wr)
    def L(r, q, sem, nbytes, fn, rd, wr): add("", r, q, 0.1, fn, rd, list(wr) + ["q" + q], sem=sem, nbytes=nbytes, lat=1.8)

    def send(st, r, to, src, dst, sem, rd, far):
        def f(g, T, topo):
            rid, pid, _ = topo.addr(T.cores[to])
            return g.remote_dma(dst(T), src(T), T.sem[sem], T.sem.sent, pid, rid, topo.mask(T.cores[r], T.cores[to]))
        add(st, r, "pool", P["ISS"], f, rd, [], sem=sem, far=[(to, far)], lat=P["SEND"])

    def cast(st, r, ap, sem, keys):
        def f(g, T, topo):
            me = T.cores[r]; to = [T.cores[(r + x) % N] for x in range(1, N)]; m = -1
            for x in to: m &= topo.mask(me, x)
            ids = [DstId(rid=topo.addr(x)[0], pnc=topo.addr(x)[1]) for x in to]
            return g.remote_dma_fused([RemoteDMATransfer(dst_ids=ids, dma_engine_mask=m, remote_sem=T.sem[sem],
                                                         srcs=[ap(T)], dsts=[ap(T)] * 3)], local_sem=T.sem.sent)
        add(st, r, "pool", P["ISS"], f, keys, [], sem=sem, far=[((r + x) % N, y) for x in range(1, N) for y in keys], lat=P["BC"])

    CST = 129.0 - 63.5 / 128.0
    CKD = 1536.0 - 64.5 / 128.0
    CMK = -2047.0 * 1535.0
    held = {}

    def setup(r):
        cur[:] = ["s", 0]
        loads = [lambda a=a, b=b: L(r, "sync", "ld%d" % (1 + a), 262144 * (b - a),
                                    lambda g, T: g.sync.dma_start(T.posi[:, 512 * a:512 * b], T.pos0[:, 512 * a:512 * b]), [], [("posi", q) for q in range(a, b)])
                 for a, b in P["POS"]]
        tabs = [lambda: L(r, "sync", "ld5", 2097152, lambda g, T: g.sync.dma_start(T.tb[:], T.tab[:]), [], [("tb", 0), ("tb", 1)])]
        L(r, "sync", "ld0", 1408, lambda g, T: g.sync.dma_start(T.ci[0:1, :], T.cand[:]), [], ["ci"])
        L(r, "act", "ld7", 32768, lambda g, T: g.scalar.dma_start(T.fi[0:64, :], T.fac[:]), [], ["fi0"])
        L(r, "act", "ld8", 32768, lambda g, T: g.scalar.dma_start(T.fi[64:128, :], T["inc"][:]), [], ["fi1"])
        L(r, "sync", "ld9", 8192, lambda g, T: g.sync.dma_start(T.thi[0:16, :], T.th[:, 512 * r:512 * r + 512]), [], ["thi"])
        for f in loads[:P["TABPOS"]] + tabs + loads[P["TABPOS"]:]: f()
        V("", r, 176, lambda g, T: g.vector.memset(T.ones[:], 1.0), [], ["ones"])
        G("", r, 128, lambda g, T: g.affine_select(T.idb[:], T.ones[:, 0:128], [[-1, 128]], A.is_equal, 0.0, 0, 1), ["ones"], ["idb"])
        G("", r, 16, lambda g, T: g.iota(T.it[:], [[-1, 16]], 128, 1), [], ["it"])
        G("", r, 352, lambda g, T: g.affine_select(T.nn[:], T.ones[:], [[0, 11], [-1, 32]], A.is_equal, 0.0, -32 * r, 1), ["ones"], ["nn"])
        V("", r, 64, lambda g, T: g.vector.tensor_scalar(T.ucol[:, 0:1], T.it[:, 0:1], -128.0, None, A.add), ["it"], ["ucol"])
        V("", r, 64, lambda g, T: g.vector.tensor_scalar(T.it2[:], T.it[:], 15, None, A.bitwise_and), ["it"], ["it2"])
        V("", r, 64, lambda g, T: g.vector.tensor_scalar(T.sel[:], T.it2[:], 0.0, None, A.is_equal), ["it2"], ["sel"])
        V("", r, 64, lambda g, T: g.vector.tensor_scalar(T.it3[:, 0:1], T.it[:, 0:1], 3, None, A.bitwise_and), ["it"], ["it3"])
        V("", r, 64, lambda g, T: g.vector.tensor_scalar(T.bcol[:, 0:1], T.it3[:, 0:1], 2048.0, None, A.mult), ["it3"], ["bcol"])
        V("", r, 64, lambda g, T: g.vector.tensor_scalar(T.bcol[:, 1:2], T.it3[:, 0:1], 2048.0, CMK, A.mult, A.add), ["it3"], ["bcol1"])
        V("", r, 128, lambda g, T: g.vector.memset(T.mf[:], 0.0), [], ["mf"])
        V("", r, 64, lambda g, T: g.vector.memset(T.land[:, 4, 4, :], 0.0), [], ["mf"])
        def idp(g, T):
            for i in range(11): x = g.scalar.activation(T.idp[:, 128 * i:128 * i + 128], T.idb[:], AF.Identity, scale=float(2 ** i))
            return x
        S("", r, 1408, idp, ["idb"], ["idp"], 11)
        V("", r, 272, lambda g, T: g.vector.memset(T.zero[:], 0.0), [], ["zero"])
        V("", r, 192, lambda g, T: g.vector.tensor_copy(T.w2[:], T.zero[:, 0:384]), ["zero"], ["w2"])
        V("", r, 70, lambda g, T: g.vector.tensor_copy(T.w4[:], T.zero[:, 0:140]), ["zero"], ["w4"])
        V("", r, 272, lambda g, T: g.vector.tensor_copy(T.mk[:], T.zero[:]), ["zero"], [("mk", x) for x in range(4)])
        S("", r, 128, lambda g, T: g.scalar.activation(T.ss[:, 352:480], T.idb[:], AF.Copy), ["idb"], ["ssi"])
        S("", r, 128, lambda g, T: g.scalar.activation(T.idf[:], T.idb[:], AF.Copy), ["idb"], ["idf"])
        V("", r, 352, lambda g, T: g.vector.tensor_copy(T.cb[0:1, :], T.ci[0:1, :]), ["ci"], ["cb"])
        def cmm(g, T):
            for i in range(11): x = g.tensor.matmul(T.pm0[:, 32 * i:32 * i + 32], T.ones[0:1, 0:128], T.cb[0:1, i:352:11], True, True)
            return x
        M("", r, 704, cmm, ["ones", "cb"], ["pm0"], 11)
        V("", r, 352, lambda g, T: g.vector.tensor_scalar(T.pm0[:, 0:352], T.pm0[:, 0:352], T.ucol[:, 0:1], None, A.is_equal), ["ucol"], ["pm0"])
        V("", r, 352, lambda g, T: g.vector.tensor_tensor(T.ss[:, 0:352], T.nn[:], T.pm0[:, 0:352], A.subtract), ["nn"], ["pm0", "ss"])
        def wmm(g, T):
            for i in range(11): x = g.tensor.matmul(T.pm1[:, 0:32], T.idp[:, 128 * i:128 * i + 128], T.ss[:, 32 * i:32 * i + 32], i == 0, i == 10)
            return x
        M("", r, 704, wmm, ["idp", "ss"], ["pm1"], 11)
        def w4(g, T):
            g.vector.tensor_scalar(T.wl[:, r, :] if P["H"] else T.w2[:, 0:8, 4:8], T.pm1[:, 0:32], -1.0, None, A.mult)
            return g.vector.tensor_scalar(T.w4[:, 3:35:4, :], T.pm1[:, 0:32], -1.0, None, A.mult)
        V("", r, 0, w4, [], ["pm1", ("wl", r) if P["H"] else "w2", "w4"], 2)
        if P["H"]: cast("", r, lambda T: T.wl[:, r, :], "wx", [("wl", r)])
        V("", r, 128, lambda g, T: g.vector.tensor_copy(T.fb[:], T.fi[:]), ["fi0", "fi1"], ["fb"])
        V("", r, 128, lambda g, T: g.vector.tensor_copy(T.thb[0:16, :], T.thi[0:16, :]), ["thi"], ["thb"])
        def fmm(g, T):
            g.tensor.matmul(T.ps0[:, 0:128], T.fb[:], T.idb[:], True, True)
            return g.tensor.matmul(T.ps0[:, 128:144], T.thb[0:16, :], T.idb[0:16, 0:16], True, True)
        M("", r, 192, fmm, ["fb", "thb", "idb"], ["ps0"], 2)
        S("", r, 144, lambda g, T: g.scalar.activation(T.ft[:], T.ps0[:, 0:144], AF.Copy), [], ["ps0", "ft"])
        def p0(g, T):
            g.scalar.activation(T.prm[:, 0:32:2], T.ft[:, 0:16], AF.Identity, scale=1.0 / 128)
            return g.scalar.activation(T.prm[:, 1:32:2], T.ft[:, 64:80], AF.Identity, scale=1.0 / 128, bias=CST)
        S("", r, 0, p0, ["ft"], ["prm"], 2)
        V("", r, 128, lambda g, T: g.vector.memset(T.cc[:], 0.0), [], ["cc"])
        V("", r, 64, lambda g, T: g.vector.memset(T.cc[:, :, 0, 1:2], 1.0), [], ["cc"])
        V("", r, 64, lambda g, T: g.vector.memset(T.rst[:], 1.0), [], ["rst"])
        V("", r, 64, lambda g, T: g.vector.memset(T.rst[:, 0:64:16], 0.0), [], ["rst"])
        V("", r, 128, lambda g, T: g.vector.memset(T.dd[:], 0.0), [], [(x, b) for x in ("dd", "dl") for b in range(2)])
        cur[:] = ["f", 0]
        def level(k):
            def f(g, T):
                for j in range(4):
                    c = 16 * k + 4 * r + j
                    x = g.scalar.activation(T.cc[:, j, 2 ** k:2 ** (k + 1), :], T.cc[:, j, 0:2 ** k, :], AF.Identity,
                                            scale=T.ft[:, c:c + 1], bias=T.ft[:, 64 + c:65 + c])
                return x
            S("tree", r, 0, f, ["ft", "cc"], ["cc"], 4)
        for k in range(3): level(k)
        V("tree", r, 128, lambda g, T: g.vector.tensor_copy(T.cj[:], T.cc[:]), ["cc"], ["cj"])
        V("tree", r, 128, lambda g, T: g.vector.tensor_scalar(T.cj[:], T.cj[:], 127, None, A.bitwise_and), ["cj"], ["cj"])
        V("tree", r, 128, lambda g, T: g.vector.tensor_copy(T.cc[:], T.cj[:]), ["cj"], ["cc"])
        level(3)
        def fa2(g, T):
            g.vector.tensor_tensor(T.cj[:, :, :, 0], T.cc[:, :, :, 1], T.cc[:, :, :, 0], A.subtract)
            return g.vector.tensor_copy(T.cj[:, :, :, 1], T.cc[:, :, :, 0])
        V("tree", r, 192, fa2, ["cc"], ["cj"], 2)
        V("tree", r, 128, lambda g, T: g.vector.tensor_scalar(T.cj[:], T.cj[:], 127, None, A.bitwise_and), ["cj"], ["cj"])
        def t0(g, T):
            g.vector.tensor_scalar(T.t0[:, :, :, 0], T.cj[:, :, :, 0], 1.0 / 128, None, A.mult)
            return g.vector.tensor_scalar(T.t0[:, :, :, 1], T.cj[:, :, :, 1], 1.0 / 128, CST, A.mult, A.add)
        V("tree", r, 0, t0, ["cj"], [("t", 0, b) for b in range(2)], 2)

    def quotients(r, tl, move, key, s, k0, pt="pt0"):
        def kq(g, T):
            for j in range(2):
                x = g.vector.tensor_scalar(T.kk[:, 256 * s + 128 * j:256 * s + 128 * j + 128], T.xd[:, tl + j, 352:480],
                                           move(T, j, 0), move(T, j, 1), A.mult, A.add)
            return x
        def ks(g, T):
            for j in range(2):
                x = g.scalar.activation(T.kk[:, 256 * s + 128 * j:256 * s + 128 * j + 128], T.xd[:, tl + j, 352:480], AF.Identity,
                                        scale=move(T, j, 0), bias=move(T, j, 1))
            return x
        if key == "prm" and tl // 4 in P["QS"]:
            S("kq", r, 256, ks, [("xd", tl), ("xd", tl + 1), key], [("kk", s)], 2)
        else:
            V("kq", r, 0, kq, [("xd", tl), ("xd", tl + 1), key], [("kk", s)], 2)
        def tr(g, T):
            for j in range(2):
                x = g.tensor.transpose(T[pt][:, k0 + 128 * j:k0 + 128 * j + 128], T.kk[:, 256 * s + 128 * j:256 * s + 128 * j + 128], T.idb[:])
            return x
        M("tr", r, 256, tr, [("kk", s), "idb"], [pt], 2)

    def gather(r, o0, w, xv, slots):
        g0 = 1024 * slots[0]; rd = [("off", o0), ("tb", 0), ("tb", 1)]
        if xv:
            V("gv", r, 16 * xv * P["GAM"], lambda g, T: g.vector.tensor_copy(T.gath[:, g0:g0 + 16 * xv], T.tb[:, 0:8192].indirect(T.off[:, o0:o0 + xv])),
              rd, [("gv", x) for x in slots])
        S("gs", r, 16 * (w - xv) * P["GAM"] + 12,
          lambda g, T: g.scalar.activation(T.gath[:, g0 + 16 * xv:g0 + 16 * w], T.tb[:, 0:8192].indirect(T.off[:, o0 + xv:o0 + w]), AF.Copy),
          rd, [("gs", x) for x in slots])
        return [(k, x) for k in ("gv", "gs") for x in slots]

    def sums(r, e, n, u, nt, got, g0):
        ps = "ps%d" % (n % 2); own = u // 2; lb = u % 2; f = 32 * lb; w = 16 * nt
        def sm(g, T):
            for j in range(nt):
                for t in range(4):
                    x = g.tensor.matmul(T[ps][:, 16 * j:16 * j + 16], T.gath[:, g0 + 4 * j + t:g0 + 512 * nt:4 * nt], T.sel[:], t == 0, t == 3)
            return x
        M("sm", r, 256 * nt, sm, got + ["sel"], [ps], 4 * nt)
        if own != r:
            src = 256 * e + 32 * u; slot = (r - own - 1) % N
            V("pa", r, 64, lambda g, T: g.vector.tensor_scalar(T.part[:, src:src + w], T[ps][:, 0:w], -1.0 if slot == 1 else 1.0, None, A.mult), [], [ps, ("part", e, u)])
            send("se", r, own, lambda T: T.part[:, src:src + w], lambda T: T.land[:, e, slot, f:f + w], "ar%d_%d" % (e, lb), [("part", e, u)], ("land", e, lb, slot))
        elif e == 0:
            V("ow", r, 64, lambda g, T: g.vector.tensor_scalar(T.land[:, 0, 3, :], T[ps][:, 0:w], -1.0, None, A.mult), [], [ps, ("own", e, lb)])
        elif e == 1:
            V("ow", r, 64, lambda g, T: g.vector.tensor_copy(T.gg[:], T[ps][:, 0:w]), [], [ps, ("gg", 0), ("gg", 1)])
        elif e < 4:
            V("ow", r, 64, lambda g, T: g.vector.tensor_tensor(T.land[:, e, 3, f:f + w], T.fa[:, f:f + w], T[ps][:, 0:w], A.subtract), [("F", lb)], [ps, ("own", e, lb)])
        elif n >= 38:
            held[r, lb] = (lambda T: T[ps][:, 0:w]), ps
        else:
            V("ow", r, 64, lambda g, T: g.vector.tensor_copy(T.ow[:, f:f + w], T[ps][:, 0:w]), [], [ps, ("ow", lb)])
            held[r, lb] = (lambda T: T.ow[:, f:f + w]), ("ow", lb)

    def first(r, q, e, n):
        cur[:] = ["f", n]; pm = "pm%d" % (n % 2)
        if e == 0:
            for u in (2 * q, 2 * q + 1):
                c = 256 * u
                if P["X0"][u] == "dve":
                    V("x0", r, 256, lambda g, T, c=c: g.vector.tensor_copy(T.x0[:, c:c + 256], T.posi[:, c:c + 256]), [("posi", q)], [("x0", u)])
                else:
                    G("x0", r, 256, lambda g, T, c=c: g.affine_select(T.x0[:, c:c + 256], T.posi[:, c:c + 256], [[0, 256]], A.is_ge, 0.0, 0, 0), [("posi", q)], [("x0", u)])
                for j in range(2):
                    tl = 2 * u + j; px = "px%d" % j
                    M("xm", r, 480, lambda g, T, tl=tl, px=px: g.tensor.matmul(T[px][:, 0:480], T.x0[:, 128 * tl:128 * tl + 128], T.ss[:], True, True),
                      [("x0", u), "ss", "ssi"], [px])
                    S("xc", r, 480, lambda g, T, tl=tl, px=px: g.scalar.activation(T.xd[:, tl, :], T[px][:, 0:480], AF.Copy), [], [px, ("xd", tl)])
        else:
            for h in range(2):
                c = 8 * q + 4 * h
                quotients(r, 4 * q + 2 * h, lambda T, j, i, c=c: T.prm[:, c + 2 * j + i:c + 2 * j + i + 1], "prm", 2 * q + h, 256 * h)
            if q in P["KS"]:
                S("kt", r, 512, lambda g, T: g.scalar.activation(T.kt[:, 512 * q:512 * q + 512], T.pt0[:, 0:512], AF.Copy), [], ["pt0", ("kt", 2 * q), ("kt", 2 * q + 1)])
            else:
                V("kt", r, 256, lambda g, T: g.vector.tensor_copy(T.kt[:, 512 * q:512 * q + 512], T.pt0[:, 0:512]), [], ["pt0", ("kt", 2 * q), ("kt", 2 * q + 1)])
        for j in range(4):
            tl = 4 * q + j
            V("kd", r, 176, lambda g, T, j=j, tl=tl: g.vector.tensor_scalar(
                T.kd4[:, n, :, j, :], T.xd[:, tl, 0:352], T.prm[:, 2 * tl:2 * tl + 1] if e else 1.0 / 128, CKD, A.mult, A.add),
              [("xd", tl)] + ["prm"] * e, [("kd4", n, j)])
        for i0, i1 in ((0, 4), (4, 8), (8, 11)):
            def mq(g, T, i0=i0, i1=i1):
                for i in range(i0, i1):
                    x = g.tensor.matmul(T[pm][:, 0:128], T.kd4[:, n, 8 * i:8 * i + 8, :, :], T.idp[:, 128 * i:128 * i + 128], i == 0, e == 0 and i == 10)
                return x
            M("mq", r, 128 * (i1 - i0), mq, [("kd4", n, j) for j in range(4)] + ["idp"], [pm], i1 - i0)
        if e:
            def wq(g, T):
                for j in range(4):
                    x = g.tensor.matmul(T[pm][:, 0:128], T.w4[:, 3 - j:35 - j, :], T.kt[:, 512 * q + 128 * j:512 * q + 128 * j + 128], False, j == 3)
                return x
            M("wq", r, 512, wq, [("kt", 2 * q), ("kt", 2 * q + 1), "w4"], [pm], 4)
        V("of", r, 128, lambda g, T: g.vector.tensor_scalar(T.off[:, 128 * n:128 * n + 128], T[pm][:, 0:128], T.bcol[:, 1:2], None, A.add),
          ["bcol1"], [pm, ("off", 128 * n)])
        sums(r, e, n, 2 * q, 4, gather(r, 128 * n, 128, P["X1"][8 * r + n], [2 * n, 2 * n + 1]), 2048 * n)

    def unit(r, e, u, n):
        cur[:] = ["u", n]
        s = n % RING; z = n % 4; c = 2 * (u % 2) if e == 2 else 0; ub = u - u % 2 if e == 2 else u
        pm, po = ("pm0", "px0")[n % 2], ("pm1", "px1")[n % 2]
        if P["H"]:
            move = lambda T, j, i: T.sx[:, e - 2, ub, c + j:c + j + 1]
        else:
            move = lambda T, j, i: T.sx[:, e - 2, u, 2 * j + i:2 * j + i + 1]; pt = "pt%d" % (n % 2)
            quotients(r, 2 * u, move, ("sx", e - 1, u), s, 0, pt)
            V("kt", r, 128, lambda g, T: g.vector.tensor_copy(T.kt[:, 256 * s:256 * s + 256], T[pt][:, 0:256]), [], [pt, ("kt", s)])
        for j in range(2):
            V("kd", r, 176, lambda g, T, j=j: g.vector.tensor_scalar(T.kd[:, s, :, j, :], T.xd[:, 2 * u + j, 0:352], move(T, j, 0), CKD, A.mult, A.add),
              [("xd", 2 * u + j), ("sx", e - 1, u)], [("kd", s, j)])
        def mq(g, T):
            for i in range(11):
                x = g.tensor.matmul(T[pm][:, 0:64], T.idp[:, 128 * i:128 * i + 128], T.kd[:, s, 8 * i:8 * i + 8, :, :], i == 0, bool(P["H"]) and i == 10)
            return x
        M("mq", r, 704, mq, [("kd", s, 0), ("kd", s, 1), "idp"], [pm], 11)
        if P["H"]:
            hq = (lambda T: T.hs[:, e - 2, u % 2, 64 * r:64 * r + 64]) if u // 2 == r else (lambda T: T.hl[:, e - 2, u, :])
            V("mc", r, 64, lambda g, T: g.vector.tensor_tensor(T.mk[:, z, 1:17:2, :], T[pm][:, 0:64], hq(T), A.add), [("hq", e - 1, u)], [pm, ("mk", z)])
        else:
            def wq(g, T):
                for j in range(2):
                    x = g.tensor.matmul(T[pm][:, 0:64], T.kt[:, 256 * s + 128 * j:256 * s + 128 * j + 128], T.w2[:, 0:8, 4 - 4 * j:12 - 4 * j], False, j == 1)
                return x
            M("wq", r, 128, wq, [("kt", s), "w2"], [pm], 2)
            V("mc", r, 64, lambda g, T: g.vector.tensor_scalar(T.mk[:, z, 1:17:2, :], T[pm][:, 0:64], CMK, None, A.add), [], [pm, ("mk", z)])
        def t2(g, T):
            for h in range(2):
                x = g.tensor.matmul(T[po][:, 0:64], T.mk[:, z, 1 - h:17 - h, :], T.idb[:, h:128:2], h == 0, h == 1)
            return x
        M("t2", r, 128, t2, [("mk", z), "idb"], [po], 2)
        o0 = 64 * n
        V("of", r, 64, lambda g, T: g.vector.tensor_scalar(T.off[:, o0:o0 + 64], T[po][:, 0:64], T.bcol[:, 0:1], None, A.add), ["bcol"], [po, ("off", o0)])
        sums(r, e, n, u, 2, gather(r, o0, 64, P["XV"][e], [n % 16]), 1024 * (n % 16))

    def share(r, e, lb):
        blk = 2 * r + lb; key = ("hq", e, blk)
        quotients(r, 2 * blk, lambda T, j, i: T.nx[:, e - 1, 2 * lb + j, i:i + 1], ("nx", e, lb), blk, 0)
        V("kt", r, 128, lambda g, T: g.vector.tensor_copy(T.kt[:, 256 * blk:256 * blk + 256], T.pt0[:, 0:256]), [], ["pt0", ("kt", blk)])
        def hm(g, T):
            for j in range(2):
                x = g.tensor.matmul(T.ph[:, 0:256], T.kt[:, 256 * blk + 128 * j:256 * blk + 128 * j + 128], T.w2[:, :, 4 - 4 * j:12 - 4 * j], j == 0, j == 1)
            return x
        M("hm", r, 512, hm, [("kt", blk), "w2"], ["ph"], 2)
        V("hc", r, 256, lambda g, T: g.vector.tensor_scalar(T.hs[:, e - 1, lb, :], T.ph[:, 0:256], CMK, None, A.add), [], ["ph", key])
        for x in range(1, N):
            to = (r + x) % N
            send("hs", r, to, lambda T, to=to: T.hs[:, e - 1, lb, 64 * to:64 * to + 64], lambda T: T.hl[:, e - 1, blk, :], "hq%d_%d" % (e, blk), [key], key)

    def decide(r, e, lbs):
        cur[:] = ["e", 2 * r + e] if e < 2 else ["d", 8 * e + order(r, e).index(2 * r + lbs[0])]
        k = e - 1; lb = lbs[0]; j0, j1 = 2 * lb, 2 * lbs[-1] + 2; f0, f1 = 16 * j0, 16 * j1; w = f1 - f0; h0 = 2 * f0
        def ks(*name): return [name + (b,) for b in lbs]
        landed = [("land", e, lb, x) for x in range(3)]
        ha, hb = (lambda T: T.h2[:, h0:h0 + w]), (lambda T: T.h2[:, h0 + w:h0 + 2 * w])
        if e == 1:
            V("o1", r, 2 * w, lambda g, T: g.vector.tensor_tensor(T.land[:, 1, 3, :], T.fa[:], T.gg[:], A.subtract), ks("F") + ks("gg"), [("own", 1, 0)])
        V("h2", r, 4 * w, lambda g, T: g.vector.tensor_tensor(T.h2[:, h0:h0 + 2 * w], T.land[:, e, 0:2, f0:f1], T.land[:, e, 2:4, f0:f1], A.add),
          landed + [("own", e, lb) if e < 4 else ("F", lb)], ks("h2"))
        if e == 0:
            V("f0", r, 2 * w, lambda g, T: g.vector.tensor_tensor(T.fa[:], ha(T), hb(T), A.subtract), ks("h2"), ks("F"))
            if P["H"]: V("ds", r, 64, lambda g, T: g.vector.tensor_copy(T.w2[:, :, 4:8], T.wl[:]), [("wl", x) for x in range(N)], ["w2"])
            return
        if e < 4:
            V("vb", r, 2 * w, lambda g, T: g.vector.tensor_tensor(T.vb[:, f0:f1], ha(T), hb(T), A.is_ge), ks("h2"), ks("vb"))
            V("dl", r, 2 * w, lambda g, T: g.vector.tensor_tensor(T.dd[:, j0:j1, 8:16, :], ha(T), hb(T), A.subtract), ks("h2"), ks("dl"))
            acc = lambda T, a, b: T.land[:, 4, 4, 4 * k + a:4 * k + b]
        else:
            mine, ps = held[r, lb]
            V("gg", r, 2 * w, lambda g, T: g.vector.tensor_tensor(T.gg[:, f0:f1], hb(T), ha(T), A.subtract), ks("h2"), ks("gg"))
            V("vb", r, w, lambda g, T: g.vector.tensor_tensor(T.vb[:, f0:f1], mine(T), T.gg[:, f0:f1], A.is_ge), ks("gg"), [ps] + ks("vb"))
            V("dl", r, w, lambda g, T: g.vector.tensor_tensor(T.dl[:, f0:f1], mine(T), T.gg[:, f0:f1], A.subtract), ks("gg"), [ps] + ks("dl"))
            acc = lambda T, a, b: T.mf[:, 76 + a:76 + b]
        V("cn", r, w, lambda g, T: g.vector.tensor_tensor_scan(T.cn[:, f0:f1], T.rst[:, 0:w], T.vb[:, f0:f1], 0.0, A.mult, A.add), ks("vb") + ["rst"], ks("cn"))
        V("ac", r, 64, lambda g, T: g.vector.tensor_tensor(acc(T, j0, j1), T.cn[:, f0 + 15:f1:16], T.ft[:, 128 + 4 * k + j0:128 + 4 * k + j1], A.is_ge),
          ks("cn") + ["ft", "mf"], ks("acc", k))
        if e == 4:
            def last(g, T):
                for j in range(j0, j1):
                    x = g.vector.tensor_scalar(T.mf[:, 16 * j:16 * j + 16], T.dl[:, 16 * j:16 * j + 16], acc(T, j, j + 1), None, A.mult)
                return x
            V("mu", r, 0, last, ks("dl") + ks("acc", k), ks("mm"), j1 - j0)
            return
        n = 2 ** (3 - k); t = "t%d" % k
        V("ds", r, 4 * n * (j1 - j0), lambda g, T: g.vector.tensor_tensor(T.dd[:, j0:j1, 1:n, :], T[t][:, j0:j1, 3:2 * n:2, :], T[t][:, j0:j1, 2:2 * n:2, :], A.subtract),
          ks("t", k), ks("dd"))
        def mul(g, T):
            for j in range(j0, j1):
                x = g.vector.tensor_scalar(T.mm[:, j, :, :], T.dd[:, j, :, :], acc(T, j, j + 1), None, A.mult)
            return x
        V("mu", r, 0, mul, ks("dd") + ks("dl") + ks("acc", k), ks("mm"), j1 - j0)
        made = [("sx", e, 2 * r + b) for b in lbs]
        if P["H"]:
            sx = lambda T: T.sx[:, k, 2 * r + lb, 0:j1 - j0]
            V("pr", r, 64, lambda g, T: g.vector.tensor_tensor(sx(T), T[t][:, j0:j1, 2, 0], T.mm[:, j0:j1, 1, 0], A.add), ks("t", k) + ks("mm"), made)
            cast("ca", r, sx, "pr%d_%d" % (e, 2 * r + lb), made)
            V("pr", r, 64, lambda g, T: g.vector.tensor_tensor(T.nx[:, k, j0:j1, :], T[t][:, j0:j1, 2, :], T.mm[:, j0:j1, 1, :], A.add), ks("t", k) + ks("mm"), ks("nx", e))
            for b in lbs: share(r, e, b)
        else:
            sx = lambda T: T.sx[:, k, 2 * r + lb:2 * r + lbs[-1] + 1, :]
            V("pr", r, 64, lambda g, T: g.vector.tensor_tensor(sx(T), T[t][:, j0:j1, 2, :], T.mm[:, j0:j1, 1, :], A.add), ks("t", k) + ks("mm"), made)
            cast("ca", r, sx, "pr%d_%d" % (e, 2 * r + lb), made)
        if k < 2:
            V("tu", r, 64, lambda g, T: g.vector.tensor_tensor(T["t%d" % (k + 1)][:, j0:j1, 2:n, :], T[t][:, j0:j1, 4:2 * n:2, :], T.mm[:, j0:j1, 2:n, :], A.add),
              ks("t", k) + ks("mm"), ks("t", k + 1))
        V("fu", r, 2 * w, lambda g, T: g.vector.tensor_tensor(T.fa[:, f0:f1] if k < 2 else T.land[:, 4, 3, f0:f1], T.fa[:, f0:f1], T.mm[:, j0:j1, 8:16, :], A.add),
          ks("mm") + ks("F"), ks("F"))

    def finish(r):
        cur[:] = ["s", 0]
        M("", r, 512, lambda g, T: g.tensor.matmul(T.px1[:, 0:128], T.land[:, 4, 3:5, :], T.idf[:], True, False),
          [("F", b) for b in range(2)] + [("acc", k, b) for k in range(3) for b in range(2)] + ["idf"], ["px1"])
        M("", r, 512, lambda g, T: g.tensor.matmul(T.px1[:, 0:128], T.mf[:], T.idf[:], False, True), [("mm", b) for b in range(2)], ["px1"])
        V("", r, 128, lambda g, T: g.vector.tensor_copy(T.ys[0:80, :], T.px1[0:80, 0:128]), [], ["px1", "ys"])
        for j in range(4):
            if j % 2 == 0:
                L(r, "sync", "out", 8192, lambda g, T, j=j: g.sync.dma_start(T.yf[:, 128 * j:128 * j + 128], T.ys[16 * j:16 * j + 16, :]), ["ys"], [])
            else:
                L(r, "act", "out", 8192, lambda g, T, j=j: g.scalar.dma_start(T.yf[:, 128 * j:128 * j + 128], T.ys[16 * j:16 * j + 16, :]), ["ys"], [])
        L(r, "sync", "out", 8192, lambda g, T: g.sync.dma_start(T.ya[:], T.ys[64:80, :]), ["ys"], [])

    def order(r, e):
        late = [2 * r, 2 * r + 1][2 - P["OWNL"]:] if e == 4 else []
        return [u for u in P["ORD"] if u not in late] + late

    for r in range(N): setup(r)
    for r in range(N):
        units = [(q, e) for q in range(N) for e in range(2)]
        if r == 0 and P["SW"]: units[:3] = [(1, 0), (0, 0), (0, 1)]
        for n, (q, e) in enumerate(units): first(r, q, e, n)
    for r in range(N):
        for e in range(2): decide(r, e, [0, 1])
    for e in range(2, 5):
        for r in range(N):
            for i, u in enumerate(order(r, e)): unit(r, e, u, 8 * e + i)
        for r in range(N):
            for lb in range(2): decide(r, e, [lb])
    for r in range(N): finish(r)
    return ops


def in_line(a, b):
    return a["eng"] == b["eng"] and a["r"] == b["r"] and (a["eng"] in ("pe", "sync") or bool(a["sem"] and b["sem"]))


def schedule(ops, P):
    n = len(ops); succ = [[] for _ in ops]; left = [len(o["deps"]) for o in ops]; dur = []
    for o in ops:
        dur.append(max(o["dur"], o["nbytes"] / P["BW"] / 1000) if o["eng"] == "sync" else o["dur"])
        for d in sorted(o["deps"]):
            succ[d].append((o["i"], 0.0 if in_line(ops[d], o) else P["HOP"] + ops[d]["lat"]))
    qu = [5 * o["r"] + QUEUES.index(o["eng"]) for o in ops]; lvl = [0.0] * n; key = [0.0] * n
    for o in reversed(ops):
        i, m, st = o["i"], o["n"], o["st"]
        lvl[i] = dur[i] + max([lvl[x] + lag for x, lag in succ[i]] + [o["lat"]])
        if st == "s": key[i] = -100.0 - lvl[i]
        else: key[i] = P["AT"][st] + (P["PA"] * m if st in EARLY else 10 + P["PB"] * m if m < 8 else P["T2"] + P["PS"] * (m - 16)) + 1e-6 * i
    ready = [0.0] * n; free = [0.0] * (5 * N); cand = [[] for _ in free]; nxt = [1e9] * (5 * N); seq = []; seen = set()
    for i in range(n):
        if not left[i]: cand[qu[i]].append(i); nxt[qu[i]] = 0.0
    for _ in range(n):
        t = min(nxt); q = nxt.index(t); c = cand[q]; lim = t + P["LA"]
        lim += P["AL"] * dur[min((i for i in c if ready[i] <= lim), key=lambda i: key[i])]
        b = min((i for i in c if ready[i] <= lim), key=lambda i: key[i]); o = ops[b]; d = dur[b]
        if o["eng"] == "pool" and o["sem"] and o["r"] not in seen: seen.add(o["r"]); d += P["FIRST"]
        c.remove(b); end = free[q] = max(t, ready[b]) + d; seq.append(b)
        nxt[q] = max(free[q], min(ready[x] for x in c)) if c else 1e9
        for x, lag in succ[b]:
            ready[x] = max(ready[x], end + lag); left[x] -= 1
            if not left[x]:
                cand[qu[x]].append(x); nxt[qu[x]] = min(nxt[qu[x]], max(free[qu[x]], ready[x]))
    return seq


def arrange(ops, P):
    n = len(ops); succ = [[] for _ in ops]; pred = [[] for _ in ops]; dur = []
    for o in ops:
        dur.append(max(o["dur"], o["nbytes"] / P["BW"] / 1000) if o["eng"] == "sync" else o["dur"])
        for d in sorted(o["deps"]):
            lag = 0.0 if in_line(ops[d], o) else P["HOP"] + ops[d]["lat"]
            succ[d].append((o["i"], lag)); pred[o["i"]].append((d, lag))
    qu = [5 * o["r"] + QUEUES.index(o["eng"]) for o in ops]

    def run(before, after, key, t0, slow):
        left = [len(x) for x in before]; ready = list(t0); free = [0.0] * (5 * N); cand = [[] for _ in free]
        nxt = [1e9] * (5 * N); seq = []; end = [0.0] * n; first = {}
        for i in range(n):
            if not left[i]: cand[qu[i]].append(i); nxt[qu[i]] = min(nxt[qu[i]], ready[i])
        for _ in range(n):
            t = min(nxt); q = nxt.index(t); c = cand[q]; lim = t + P["LA"]
            lim += P["AL"] * dur[min((i for i in c if ready[i] <= lim), key=lambda i: key[i])]
            b = min((i for i in c if ready[i] <= lim), key=lambda i: key[i])
            if slow is None and ops[b]["eng"] == "pool" and ops[b]["sem"]: first.setdefault(q, b)
            d = dur[b] + P["FIRST"] * (b in slow if slow else first.get(q) == b)
            c.remove(b); end[b] = free[q] = max(t, ready[b]) + d; seq.append(b)
            nxt[q] = max(free[q], min(ready[x] for x in c)) if c else 1e9
            for x, lag in after[b]:
                ready[x] = max(ready[x], end[b] + lag); left[x] -= 1
                if not left[x]:
                    cand[qu[x]].append(x); nxt[qu[x]] = min(nxt[qu[x]], max(free[qu[x]], ready[x]))
        return seq, end, set(first.values())

    key = [0.0] * n
    for i in reversed(range(n)): key[i] = min([key[x] - lag for x, lag in succ[i]] + [-ops[i]["lat"]]) - dur[i]
    for _ in range(P["IT"]):
        seq, end, slow = run(pred, succ, key, [0.0] * n, None)
        key = [-x for x in run(succ, pred, [-x for x in end], [o["lat"] for o in ops], slow)[1]]
    return seq


PLAN = {}


def rank_program(g, core, T, topo):
    r = T.rank_of(core)
    if r is None:
        return
    if not PLAN:
        PLAN["ops"] = build(P); PLAN["seq"] = arrange(PLAN["ops"], P)
    ops, seq = PLAN["ops"], PLAN["seq"]
    Q = {"pe": g.tensor, "dve": g.vector, "act": g.scalar, "pool": g, "sync": g.sync}
    mine = [ops[i] for i in seq if ops[i]["r"] == r]

    def engines(o, dst):
        return len(topo.engines(T.cores[o["r"]], T.cores[dst]))
    total = {}
    for i in set(d for o in mine for d in o["deps"] if ops[d]["r"] != r):
        total[ops[i]["sem"]] = total.get(ops[i]["sem"], 0) + engines(ops[i], r)
    pos = {o["i"]: k for k, o in enumerate(mine)}
    know = {q: {} for q in Q}; after = {}; waits = {}; marked = set()
    for o in mine:
        kn = know[o["eng"]]; w = []
        for d in sorted((ops[x] for x in o["deps"]), key=lambda d: (-pos.get(d["i"], -1), d["i"])):
            if in_line(d, o): continue
            if d["r"] == r and d["eng"] == "pool" and d["sem"]: continue
            key = d["sem"] or d["eng"]; val = pos[d["i"]] if not d["sem"] else 0
            if kn.get(key, -1) >= val: continue
            w.append(d); kn[key] = val
            if not d["sem"]:
                marked.add(d["i"])
                for k2, v2 in after[d["i"]].items():
                    if kn.get(k2, -1) < v2: kn[k2] = v2
        waits[o["i"]] = w; after[o["i"]] = dict(kn)
    count = {q: 0 for q in Q}; at = {}; sent = 0; outs = 0
    for o in mine:
        q = Q[o["eng"]]
        for d in waits[o["i"]]:
            if d["r"] != r: q.wait_ge(T.sem[d["sem"]], total[d["sem"]])
            elif d["sem"]: q.wait_ge(T.sem[d["sem"]], 16)
            else: q.wait_ge(T.sem[d["eng"]], at[d["i"]])
        if o["eng"] == "pool" and o["sem"]:
            o["fn"](g, T, topo); sent += engines(o, (r + 1) % N)
        elif o["sem"]:
            o["fn"](g, T).then_inc(T.sem[o["sem"]], 16); outs += 16 * (o["sem"] == "out")
        else:
            x = o["fn"](g, T)
            if o["i"] in marked:
                x.then_inc(T.sem[o["eng"]], 1); count[o["eng"]] += 1; at[o["i"]] = count[o["eng"]]
    g.wait_ge(T.sem.sent, sent)
    g.sync.wait_ge(T.sem.out, outs)
